import numpy as np, ml_dtypes
CORES = [25,29,65,69,153,157,193,197]
N = 8
import mx_ref
BF = ml_dtypes.bfloat16
def pick(q, e):
    c = np.concatenate([q[0].reshape(128, -1, 4), np.zeros((128, 1, 4), np.uint8)], axis=1); s = np.concatenate([q[1], np.ones((16, 1), np.uint8)], axis=1)
    return (np.ascontiguousarray(c[:, e].reshape(128, -1)), np.ascontiguousarray(s[:, e]))
def join(*qs):
    return (np.concatenate([q[0] for q in qs], axis=1), np.concatenate([q[1] for q in qs], axis=1))
def put(q, e, v):
    c, s = q[0].reshape(128, -1, 4).copy(), q[1].copy(); c[:, e] = v[0].reshape(128, -1, 4); s[:, e] = v[1]
    return (c.reshape(128, -1), s)
def pk(c, s):
    return (np.ascontiguousarray(c), mx_ref.live(s))
def emit(q):
    return q[0], q[1]
def decode(q):
    o = []
    for b in range(4):
        e = np.zeros((128, 128, 4), np.float32); e[np.arange(128), np.arange(128), b] = 1
        o.append(mx_ref.matmul(mx_ref.quantize(e.reshape(128, 512).astype(BF)), q))
    return np.stack(o, axis=2).reshape(128, -1)
def f(rng, *shape):
    return mx_ref.flush((rng.standard_normal(shape, dtype=np.float32) * np.exp2(rng.integers(-2, 3, shape[:-1] + (1,)))).astype(BF))
def wide(rng, *shape, cols=0):
    v = rng.standard_normal(shape, dtype=np.float32) * np.exp2(rng.integers(-12, 13, shape)).astype(np.float32)
    if cols: v *= np.repeat(np.exp2(rng.integers(-cols, cols + 1, shape[:-2] + (1, shape[-1] // 4))) * (rng.random(shape[:-2] + (1, shape[-1] // 4)) > 0.0625), 4, axis=-1).astype(np.float32)
    return mx_ref.flush(v.astype(BF))
T, CAPP = 128, 32
def quads(q, e):
    c = np.concatenate([q[0].reshape(128, -1, 4), np.zeros((128, 1, 4), np.uint8)], axis=1); s = np.concatenate([q[1], np.ones((16, 1), np.uint8)], axis=1)
    return (np.concatenate([c[32 * h:32 * h + 32][:, e[h]] for h in range(4)]).reshape(128, -1), np.concatenate([s[4 * h:4 * h + 4][:, e[h]] for h in range(4)]))
def level(b, z):
    n, e = z[1].shape[1], []
    for h in range(4):
        only = np.where(np.arange(4)[:, None] == h, np.arange(n)[None, :], -1)
        e.append(np.argmax(mx_ref.matmul(b, quads(z, only)) + np.float32(0), axis=0))
    e = np.stack(e)
    return e, quads(b, e)
def big(v):
    v = v.astype(np.float32)
    v[np.abs(v) < np.float32(2.0 ** -16)] = 0
    return v.astype(BF)
def coarse(v):
    v = v.copy()
    v[:, N:] = 0
    return np.stack([v.reshape(128, 512)] * N)
def planted(rng, cell, low=False):
    at = rng.permutation(N)[np.arange(128) // (128 // N)]
    c = (1 + rng.random((128, 128, 4))) * (at[:, None] == np.arange(128)[None, :])[:, :, None]
    on = at[None, :, None] == cell[:, None, :]
    v = np.where(on[:, :, :, None], 8 + 8 * rng.random((N, 128, T, 4)), 2 * rng.random((N, 128, T, 4)) - 1)
    if low:
        u = 1 + rng.random((N, 128, T // 2, 4))
        v[:, :, 1::2] = np.where(on[:, :, 1::2, None], -0.5 * u, -8 * u)
        c = c * 2.0 ** 20
    v = v * np.exp2(rng.integers(-3, 4, (N, 1, T, 1)))
    return {"x": big(v.reshape(N, 128, 4 * T)), "co": coarse(big(c))}
def setup_inputs(rng):
    return {"x": big(f(rng, N, 128, 4 * T)), "co": coarse(big(f(rng, 128, 512)).reshape(128, 128, 4)), "b1": big(f(rng, N, 128, 512)), "b2": big(f(rng, N, 128, 512)), "w": f(rng, N, 128, 512)}
def setup_inputs_spread(rng):
    d = setup_inputs(rng)
    d["x"], d["b1"] = big(wide(rng, N, 128, 4 * T, cols=6)), big(wide(rng, N, 128, 512))
    return d
def setup_inputs_ties(rng):
    d = setup_inputs(rng)
    for k in ("b1", "b2"):
        b = d[k].reshape(N, 128, 128, 4).copy()
        for r in range(N):
            for h in range(4): b[r, 32 * h:32 * h + 32] = b[r, 32 * h:32 * h + 32][:, rng.permutation(128) % 32]
        d[k] = b.reshape(N, 128, 512)
    c = d["co"][0].reshape(128, 128, 4).copy()
    c[:, :N] = c[:, rng.permutation(N) % (N // 2)]
    d["co"] = coarse(c)
    return d
def setup_inputs_crowd(rng):
    g, cell = int(rng.integers(0, N)), []
    for s in range(N):
        o = rng.permutation(np.delete(np.arange(N), g))
        if o[0] == s: o = o[::-1]
        m = int(rng.integers(1, 17))
        cell.append(rng.permutation(np.concatenate([np.full(CAPP + m, g), np.full(CAPP, o[0]), o[1:][rng.integers(0, N - 2, T - 2 * CAPP - m)]])))
    return {**setup_inputs(rng), **planted(rng, np.stack(cell))}
def setup_inputs_few(rng):
    g, a, b = [int(i) for i in rng.permutation(N)[:3]]
    cell = np.delete(np.arange(N), g)[rng.integers(0, N - 1, (N, T))]
    cell[a], cell[b] = a, a
    return {**setup_inputs(rng), **planted(rng, cell, low=True)}
def setup_inputs_zero(rng):
    d, h = setup_inputs(rng), [int(i) for i in rng.permutation(4)]
    neg, pat, gap = [slice(32 * i, 32 * i + 32) for i in h[:3]]
    p = (1 + rng.random((32, 1, 4))) * np.exp2(rng.integers(-2, 3, (32, 1, 1)))
    v, b, c = d["x"].astype(np.float32).reshape(N, 128, T, 4), d["b1"].astype(np.float32).reshape(N, 128, 128, 4), d["co"][0].reshape(128, 128, 4).copy()
    u = d["b2"].astype(np.float32)
    c[neg], c[pat] = 0, 0
    c[:, int(rng.integers(0, N))] = 0
    v[:, neg], b[:, neg], u[:, neg] = -np.abs(v[:, neg]), np.abs(b[:, neg]), np.abs(u[:, neg])
    v[:, pat] = p
    for r in range(N):
        e, k = rng.permutation(T), rng.integers(0, 4, 128)
        v[r, gap][:, e[T // 8:T // 2]] = 0
        v[r][:, e[:T // 8]] = 0
        k[int(rng.integers(0, 128))] = 0
        b[r, pat] = p * np.exp2(-k.astype(np.float64))[:, None]
        if r % 2 == 0: b[r, neg, int(rng.integers(0, 128))] = 0
    k = np.float32(2.0 ** 20)
    d["x"], d["b1"], d["b2"], d["co"] = big(v.reshape(N, 128, 4 * T) * k), big(b.reshape(N, 128, 512) * k), big(u * k), coarse(c)
    return d
def check_inputs(d):
    b = []
    for k in ("x", "co", "b1", "b2", "w"):
        v = np.abs(d[k].astype(np.float32))
        if not (np.isfinite(v).all() and ((v == 0) | (v >= 2.0 ** -30) & (v <= 2.0 ** 30)).all()): b.append("a value of " + k)
    c = d["co"].astype(np.float32)
    if (c[:, :, 4 * N:] != 0).any(): b.append("co has numbers behind its first N columns")
    if (c != c[:1]).any(): b.append("co isn't the same on all ranks")
    return b
def reference(x, co, b1, b2, w):
    oc, osc = np.zeros((N, 128, 8 * T), np.uint8), np.zeros((N, 16, 2 * T), np.uint8)
    wn, y = np.full((N, 8, T), -1, np.float32), np.zeros((N, 128, T), np.float32)
    q = [mx_ref.quantize(x[s]) for s in range(N)]
    taken = np.full((N, N, CAPP), -1)
    for s in range(N):
        cell = np.argmax(mx_ref.matmul(mx_ref.quantize(co[s]), q[s])[:N] + np.float32(0), axis=0)
        for d in range(N):
            t = np.flatnonzero(cell == d)[:CAPP]
            taken[s, d, :len(t)] = t
    home = [pick(q[s], np.full(2 * T, -1)) for s in range(N)]
    for d in range(N):
        z = join(*[pick(q[s], taken[s, d]) for s in range(N)])
        n1, v1 = level(mx_ref.quantize(b1[d]), z)
        r = mx_ref.quantize((decode(z) - decode(v1)).astype(BF))
        n2, v2 = level(mx_ref.quantize(b2[d]), r)
        for s in range(N):
            k = np.flatnonzero(taken[s, d] >= 0)
            t, i = taken[s, d][k], s * CAPP + k
            wn[s, :4, t], wn[s, 4:, t] = n1[:, i].T, n2[:, i].T
            home[s] = put(put(home[s], t, pick(v1, i)), T + t, pick(v2, i))
    for s in range(N):
        oc[s], osc[s] = emit(home[s])
        m = mx_ref.matmul(mx_ref.quantize(w[s]), home[s])
        y[s] = m[:, :T] + m[:, T:]
    return {"oc": oc, "osc": osc, "wn": wn, "y": y}

@@ -1,0 +1,591 @@
+from concourse.bass import DstId, RemoteDMATransfer
+from concourse.mybir import dt, AluOpType, AxisListType, ActivationFunctionType
+
+OP = AluOpType
+AF = ActivationFunctionType
+F8 = "float8_e4m3fn_x4"
+
+SCRATCH = {}
+
+
+def _codes(name, n):
+    SCRATCH[name] = ("sbuf", [128, n], F8)
+    SCRATCH[name + "_s"] = ("sbuf", [128, n], "uint8")
+
+
+def _buf(name, n, ty="float32"):
+    SCRATCH[name] = ("sbuf", [128, n], ty)
+
+
+for _n, _w in (("qx", 256), ("qc", 128), ("qr", 128), ("qb1", 128), ("qb2", 128), ("qw", 128), ("qe", 512), ("qm", 512),
+               ("sf", 128), ("sn", 128), ("zn", 256), ("zf", 256), ("dg1n", 512), ("dg1f", 512), ("dg2n", 512), ("dg2f", 512),
+               ("v1n", 128), ("v1f", 128), ("v2n", 128), ("v2f", 128), ("rqn", 256), ("rqf", 256),
+               ("lv1", 384), ("lv2", 384), ("h1", 128), ("h2", 128), ("rz", 64), ("rv1", 64), ("rv2", 64)):
+    _codes(_n, _w)
+for _n, _w in (("xt", 512), ("ct", 512), ("b1t", 512), ("b2t", 512), ("wt", 512), ("zt", 512), ("onb", 520), ("gp", 520), ("gm", 520),
+               ("le", 128), ("oh", 128), ("ohf", 128), ("inc", 128), ("cmp", 384), ("jk", 512), ("rtn", 512), ("rtf", 512),
+               ("xw", 512), ("xtw", 576)):
+    _buf(_n, _w, "bfloat16")
+for _n, _w in (("rst", 128), ("ts", 128), ("pm0", 128), ("pmn", 512), ("pmf", 512), ("cf", 32), ("kb0", 8), ("kb", 8),
+               ("la0", 32), ("hp", 32), ("mk", 32), ("a2", 32), ("a3", 32), ("cnt", 8), ("x0", 32), ("xt0", 32), ("y0", 16),
+               ("t1", 128), ("t2", 128), ("t3", 128), ("t4", 128), ("sl", 4),
+               ("nnn", 8), ("nnf", 8), ("rn", 4), ("lan", 16), ("wnt", 256), ("yt", 128),
+               ("xsn", 128), ("xsf", 128), ("xsh", 128)):
+    _buf(_n, _w)
+_buf("ip", 1, "int32")
+_buf("ic", 8, "int32")
+for _n, _w in (("oco", 8), ("offd", 32), ("offs", 16), ("offh", 8), ("off1n", 8), ("off1f", 8), ("off2n", 8), ("off2f", 8)):
+    _buf(_n, _w, "uint16")
+SCRATCH["sc"] = ("psum", [128, 2048], "float32")
+SCRATCH["dd"] = ("psum", [128, 2048], "float32")
+
+SEMAPHORES = (["ev", "es", "et", "ep", "sent", "st"] + ["l%d" % i for i in range(20)]
+              + ["azn", "azf", "hv1n", "hv1f", "hv2n", "hv2f", "hnn", "hnf"]
+              + ["rzc", "rzs", "r1c", "r1s", "rnc", "r2c", "r2s"])
+
+VS = 5
+FN = 4
+FF = 4
+FB = 8
+FR = 4
+BIG = -9e29
+
+
+def plan(T, topo, core):
+    cs = list(T.cores)
+    here = [c for c in cs if c in topo.cores_of(core)]
+    plane = [c for c in cs if c not in here and topo.same_plane(core, c)]
+    far = [c for c in cs if c not in here and c not in plane]
+    g0 = [c for c in far if c in topo.cores_of(far[0])]
+    g1 = [c for c in far if c not in g0]
+    rel = [c for c in topo.cores_of(core) if c not in cs and topo.die(c) == topo.die(core)
+           and all(topo.may_write(c, d) for d in far)]
+    rk = T.rank_of
+    return {"near": [[rk(c) for c in plane], [rk(c) for c in here]], "far": [[rk(c) for c in g0], [rk(c) for c in g1]],
+            "relays": rel[:2]}
+
+
+def bits(es):
+    m = 0
+    for e in es:
+        m |= 1 << e
+    return m
+
+
+def rank_program(g, core, T, topo):
+    if T.rank_of(core) is None:
+        relay_program(g, core, T, topo)
+    else:
+        home_program(g, core, T, topo)
+
+
+def xfer(T, topo, src, dst, engs, sem, out, in_):
+    rid, pid = topo.addr(dst, src)
+    return RemoteDMATransfer(dst_ids=[DstId(rid=rid, pnc=pid)], dma_engine_mask=bits(engs), remote_sem=T.sem[sem], src=in_, dst=out)
+
+
+def u8(T, name, a, b):
+    return T[name][:, a:b].bitcast(dt.uint8)
+
+
+def relay_program(g, core, T, topo):
+    src, grp = None, None
+    for c in T.cores:
+        if c in topo.cores_of(core):
+            p = plan(T, topo, c)
+            for i in range(2):
+                if p["relays"][i] == core:
+                    src, grp = T.rank_of(c), p["far"][i]
+    if src is None:
+        return
+    sent = [0]
+
+    def hand(wait, n, sem, mk):
+        ts = []
+        g.wait_ge(T.sem[wait], n)
+        for j, d in enumerate(grp):
+            dst = T.cores[d]
+            es = topo.engines(core, dst)[FR * j:FR * j + FR]
+            pd = plan(T, topo, dst)
+            at = (pd["far"][0] + pd["far"][1]).index(src)
+            out, in_ = mk(j, at)
+            ts.append(xfer(T, topo, core, dst, es, sem, out, in_))
+            sent[0] += FR
+        g.remote_dma_fused(ts, local_sem=T.sem.sent)
+
+    hand("rzc", FF, "azf", lambda j, at: (u8(T, "zf", 32 * at, 32 * at + 32), u8(T, "rz", 32 * j, 32 * j + 32)))
+    hand("rzs", FF, "azf", lambda j, at: (T["zf_s"][:, 32 * at:32 * at + 32], T["rz_s"][:, 32 * j:32 * j + 32]))
+    o = 32 * src
+    hand("r1c", FB, "hv1f", lambda j, at: (u8(T, "lv1", o, o + 32), u8(T, "rv1", 32 * j, 32 * j + 32)))
+    hand("r1s", FB, "hv1f", lambda j, at: (T["lv1_s"][:, o:o + 32], T["rv1_s"][:, 32 * j:32 * j + 32]))
+    hand("rnc", FB, "hnf", lambda j, at: (T["lan"][:, 2 * src:2 * src + 2], T["rn"][:, 2 * j:2 * j + 2]))
+    hand("r2c", FB, "hv2f", lambda j, at: (u8(T, "lv2", o, o + 32), u8(T, "rv2", 32 * j, 32 * j + 32)))
+    hand("r2s", FB, "hv2f", lambda j, at: (T["lv2_s"][:, o:o + 32], T["rv2_s"][:, 32 * j:32 * j + 32]))
+    g.wait_ge(T.sem.sent, sent[0])
+
+
+def home_program(g, core, T, topo):
+    me = T.rank_of(core)
+    pl = plan(T, topo, core)
+    queue = {"v": g.vector, "s": g.scalar, "t": g.tensor, "p": g, "y": g.sync}
+    engsem = {"v": "ev", "s": "es", "t": "et", "p": "ep"}
+    known = {e: {} for e in queue}
+    count = {e: 0 for e in queue}
+    total, waited, hist = {}, {}, {}
+    PS = ("sc", "dd")
+
+    def clash(a, b):
+        if a[1] >= b[2] or b[1] >= a[2]:
+            return False
+        s, t = (a[3] if len(a) > 3 else 1), (b[3] if len(b) > 3 else 1)
+        if s > 1 and s == t and a[1] % s != b[1] % s:
+            return False
+        return True
+
+    def need(e, reads, writes):
+        deps = []
+        for rs, wr in ((reads, False), (writes, True)):
+            for r in rs:
+                ps = r[0] in PS
+                for (q, qw, qe, ev, clk) in hist.get(r[0], []):
+                    if (wr or qw or (ps and qe != e)) and clash(r, q):
+                        if ps and e == "t" and qe == "t":
+                            continue
+                        deps.append((ev, clk))
+        best = {}
+        for ev, clk in deps:
+            if known[e].get(ev[0], 0) < ev[1] and (ev[0] not in best or best[ev[0]][0] < ev[1]):
+                best[ev[0]] = (ev[1], clk)
+        for s in list(best):
+            v = best[s][0]
+            if any(o != s and best[o][1].get(s, 0) >= v for o in best):
+                del best[s]
+        for s, (v, clk) in best.items():
+            queue[e].wait_ge(T.sem[s], v)
+            waited[s] = max(waited.get(s, 0), v)
+            for k2, v2 in clk.items():
+                known[e][k2] = max(known[e].get(k2, 0), v2)
+            known[e][s] = max(known[e].get(s, 0), v)
+
+    def note(e, reads, writes, ev, clk):
+        for r in reads:
+            hist.setdefault(r[0], []).append((r, False, e, ev, clk))
+        for r in writes:
+            hist.setdefault(r[0], []).append((r, True, e, ev, clk))
+
+    def op(e, call, reads, writes):
+        need(e, reads, writes)
+        count[e] += 1
+        ev = (engsem[e], count[e])
+        call().then_inc(T.sem[ev[0]], 1)
+        total[ev[0]] = count[e]
+        clk = dict(known[e])
+        clk[ev[0]] = ev[1]
+        note(e, reads, writes, ev, clk)
+
+    nl = [0]
+
+    def dma(e, out, in_, reads, writes, store=False):
+        need(e, reads, writes)
+        if store:
+            s = "st"
+        else:
+            s = "l%d" % nl[0]
+            nl[0] += 1
+        total[s] = total.get(s, 0) + 16
+        queue[e].dma_start(out, in_).then_inc(T.sem[s], 16)
+        if not store:
+            clk = dict(known[e])
+            clk[s] = 16
+            note(e, reads, writes, (s, 16), clk)
+
+    def arrive(sem, n, writes):
+        total[sem] = n
+        note("r", [], writes, (sem, n), {sem: n})
+
+    def fused(reads, parts):
+        need("p", reads, [])
+        ts = [xfer(T, topo, core, d, es, sem, out, in_) for (d, es, sem, out, in_) in parts]
+        total["sent"] = total.get("sent", 0) + sum(len(p[1]) for p in parts)
+        g.remote_dma_fused(ts, local_sem=T.sem.sent)
+
+    def ap(r):
+        return T[r[0]][:, r[1]:r[2]:r[3]] if len(r) > 3 and r[3] > 1 else T[r[0]][:, r[1]:r[2]]
+
+    def isr(x):
+        return isinstance(x, tuple)
+
+    def vcopy(o, i):
+        op("v", lambda: g.vector.tensor_copy(ap(o), ap(i)), [i], [o])
+
+    def vset(o, c):
+        op("v", lambda: g.vector.memset(ap(o), c), [], [o])
+
+    def vts(o, i, s1, s2, op0, op1=None):
+        rd = [i] + [s for s in (s1, s2) if isr(s)]
+        a1 = ap(s1) if isr(s1) else s1
+        a2 = ap(s2) if isr(s2) else s2
+        if op1 is None:
+            op("v", lambda: g.vector.tensor_scalar(ap(o), ap(i), a1, None, op0), rd, [o])
+        else:
+            op("v", lambda: g.vector.tensor_scalar(ap(o), ap(i), a1, a2, op0, op1), rd, [o])
+
+    def vtt(o, a, b, o0):
+        op("v", lambda: g.vector.tensor_tensor(ap(o), ap(a), ap(b), o0), [a, b], [o])
+
+    def vscan(o, d0, d1, init, o0, o1):
+        op("v", lambda: g.vector.tensor_tensor_scan(ap(o), ap(d0), ap(d1), init, o0, o1), [d0, d1], [o])
+
+    def vtr(o, i):
+        op("v", lambda: g.vector.transpose(ap(o), ap(i)), [i], [o])
+
+    def vsum(o, i):
+        op("v", lambda: g.vector.tensor_reduce(ap(o), ap(i), AxisListType.X, OP.add), [i], [o])
+
+    def quant(o, n0, i):
+        w = (i[2] - i[1]) // 4
+        a, b = (o, n0, n0 + w), (o + "_s", n0, n0 + w)
+        op("v", lambda: g.vector.quantize_mx(ap(a), ap(b), ap(i)), [i], [a, b])
+
+    def act(o, i, f, bias=None, scale=None, acc=None):
+        rd, kw, wr = [i], {}, [o]
+        if bias is not None:
+            kw["bias"] = ap(bias) if isr(bias) else bias
+            if isr(bias):
+                rd.append(bias)
+        if scale is not None:
+            kw["scale"] = ap(scale) if isr(scale) else scale
+            if isr(scale):
+                rd.append(scale)
+        if acc is not None:
+            kw["accum_out"] = ap(acc)
+            wr.append(acc)
+        op("s", lambda: g.scalar.activation(ap(o), ap(i), f, **kw), rd, wr)
+
+    def pick_codes(o, o0, win, w1, off, c0, c1):
+        oc, wc, of = (o, o0, o0 + 16 * (c1 - c0)), (win, 0, w1), (off, c0, c1)
+        op("v", lambda: g.vector.tensor_copy(ap(oc).bitcast(dt.uint32), ap(wc).bitcast(dt.uint32).indirect(ap(of))), [wc, of], [oc])
+
+    def pick_scales(o, o0, win, w1, off, c0, c1):
+        osn, ws, of = (o + "_s", o0, o0 + 16 * (c1 - c0)), (win + "_s", 0, w1), (off, c0, c1)
+        op("s", lambda: g.scalar.activation(ap(osn), ap(ws).indirect(ap(of)), AF.Copy), [ws, of], [osn])
+
+    def pick(*a):
+        pick_codes(*a)
+        pick_scales(*a)
+
+    def mm(ps, bank, l, l0, r, r0, start=True, stop=True):
+        o = (ps, 512 * bank, 512 * bank + 128)
+        a, sa, b, sb = (l, l0, l0 + 128), (l + "_s", l0, l0 + 128), (r, r0, r0 + 128), (r + "_s", r0, r0 + 128)
+        op("t", lambda: g.tensor.matmul_mx(ap(o), ap(a), ap(sa), ap(b), ap(sb), start, stop), [a, sa, b, sb], [(ps, 512 * bank, 512 * bank + 512)])
+
+    dma("y", T.xt[:], T.x[:], [], [("xt", 0, 512)])
+    dma("s", T.ct[:, 0:32], T.co[:, 0:32], [], [("ct", 0, 32)])
+    dma("y", T.b1t[:], T.b1[:], [], [("b1t", 0, 512)])
+    dma("y", T.b2t[:], T.b2[:], [], [("b2t", 0, 512)])
+    dma("y", T.wt[:], T.w[:], [], [("wt", 0, 512)])
+
+    near, far = pl["near"][0] + pl["near"][1], pl["far"][0] + pl["far"][1]
+    own = near.index(me)
+
+    def both(n, a, b):
+        return [(n, a, b), (n + "_s", a, b)]
+
+    nw, hw1, hw2, nn_ = [], [], [], []
+    for k, r in enumerate(near):
+        if r != me:
+            nw += both("zn", 32 * k, 32 * k + 32)
+            hw1 += both("lv1", 32 * r, 32 * r + 32)
+            hw2 += both("lv2", 32 * r, 32 * r + 32)
+            nn_.append(("lan", 2 * r, 2 * r + 2))
+    arrive("azn", 3 * 2 * FN, nw)
+    arrive("hv1n", 3 * 2 * FN, hw1)
+    arrive("hv2n", 3 * 2 * FN, hw2)
+    arrive("hnn", 3 * FN, nn_)
+    arrive("azf", 4 * 2 * FR, both("zf", 0, 128))
+    hw1, hw2, nn_ = [], [], []
+    for r in far:
+        hw1 += both("lv1", 32 * r, 32 * r + 32)
+        hw2 += both("lv2", 32 * r, 32 * r + 32)
+        nn_.append(("lan", 2 * r, 2 * r + 2))
+    arrive("hv1f", 4 * 2 * FR, hw1)
+    arrive("hv2f", 4 * 2 * FR, hw2)
+    arrive("hnf", 4 * FR, nn_)
+
+    def iota(o, pat, base, cm):
+        if o[0] == "ip":
+            op("p", lambda: g.iota(ap(o), pat, base, cm), [], [o])
+        else:
+            op("p", lambda: g.iota(ap(o), pat, base, cm, allow_small_or_imprecise_dtypes=True), [], [o])
+
+    iota(("ip", 0, 1), [[1, 1]], 0, 1)
+    iota(("kb0", 0, 8), [[2, 8]], 0, 0)
+    iota(("onb", 0, 520), [[0, 520]], 1, 0)
+    iota(("la0", 0, 32), [[32, 4], [0, 4], [16, 2]], -128, 0)
+    iota(("hp", 0, 32), [[0, 4], [1, 4], [0, 2]], 0, 0)
+    op("p", lambda: g.affine_select(T.gp[:, 0:520], T.onb[:, 0:520], [[-1, 520]], OP.is_equal, 0.0, 3, 4),
+       [("onb", 0, 520)], [("gp", 0, 520)])
+    vset(("ct", 32, 512), 0.0)
+    P1 = ("ip", 0, 1)
+    for k, (sh, m) in enumerate(((0, 15), (5, 7), (0, 7), (3, 1), (4, 1), (1, 7))):
+        o = ("ic", k, k + 1)
+        if sh:
+            vts(o, P1, sh, m, OP.arith_shift_right, OP.bitwise_and)
+        else:
+            vts(o, P1, m, None, OP.bitwise_and)
+    vset(("zt", 0, 512), 0.0)
+    vcopy(("cf", 0, 6), ("ic", 0, 6))
+
+    def C(k):
+        return ("cf", k, k + 1)
+    R16, HQ, D8, U0, U1, VV = [C(k) for k in range(6)]
+    M0, E0, KC, AL, BE, T0, MU, DC = [C(k) for k in range(8, 16)]
+    vts(("oco", 0, 8), ("zt", 0, 8), D8, None, OP.add)
+    quant("qc", 0, ("ct", 0, 512))
+    pick("qr", 0, "qc", 128, "oco", 0, 8)
+    vset(("rst", 0, 128), 0.0)
+    vset(("rst", 0, 128, 8), BIG)
+    vts(M0, U0, -1.0, 1.0, OP.mult, OP.add)
+    vts(T0, U1, 16.0, 0.5, OP.mult, OP.add)
+    vtt(KC, T0, U0, OP.add)
+    vts(("kb", 0, 8), ("kb0", 0, 8), KC, None, OP.add)
+
+    quant("qx", 0, ("xt", 0, 512))
+    mm("sc", 0, "qr", 0, "qx", 0)
+    quant("qx", 128, ("zt", 0, 512))
+    vtr(("ts", 0, 128), ("sc", 0, 128))
+    vscan(("pm0", 0, 128), ("rst", 0, 128), ("ts", 0, 128), 0.0, OP.add, OP.max)
+    for b in range(4):
+        vts(("le", 32 * b, 32 * b + 32), ("pm0", 32 * b, 32 * b + 32), ("pm0", 32 * b + 7, 32 * b + 8), None, OP.is_ge)
+    vtt(("oh", 1, 128), ("le", 1, 128), ("le", 0, 127), OP.subtract)
+    vcopy(("oh", 0, 128, 8), ("le", 0, 128, 8))
+    vtr(("ohf", 0, 128), ("oh", 0, 128))
+    vscan(("inc", 0, 128), ("onb", 0, 128), ("ohf", 0, 128), 0.0, OP.mult, OP.add)
+    for v in range(VS):
+        act(("jk", 128 * (v % 4), 128 * (v % 4) + 128), ("inc", 0, 128), AF.Sign, bias=("kb", v, v + 1), scale=-1.0, acc=("cnt", v, v + 1))
+    for v in range(VS, 8):
+        c = ("cmp", 128 * (v - VS), 128 * (v - VS) + 128)
+        vts(c, ("inc", 0, 128), ("kb", v, v + 1), None, OP.is_le)
+    for v in range(VS, 8):
+        vsum(("cnt", v, v + 1), ("cmp", 128 * (v - VS), 128 * (v - VS) + 128))
+    vts(BE, VV, float(VS), 64.0, OP.is_lt, OP.mult)
+    vts(AL, BE, -1.0 / 128, 1.0, OP.mult, OP.add)
+    for e in range(2):
+        act(("x0", 16 * e + 1, 16 * e + 16, 2), ("cnt", 0, 8), AF.Copy, scale=U0)
+        vts(("x0", 16 * e, 16 * e + 16, 2), ("cnt", 0, 8), M0, None, OP.mult)
+    vtr(("xt0", 0, 32), ("x0", 0, 32))
+    for u in range(2):
+        vtt(("y0", u, 16, 2), ("xt0", 16 * u, 16 * u + 8), ("xt0", 16 * u + 8, 16 * u + 16), OP.add)
+    vts(("offs", 0, 16), ("y0", 0, 16), AL, BE, OP.mult, OP.add)
+
+    def to_relays(buf, w, dstbuf, sem, ne):
+        codes = SCRATCH[buf][2] == F8
+        parts = []
+        for i, rc in enumerate(pl["relays"]):
+            es = topo.engines(core, rc)[(16 - 2 * ne) + ne * i:(16 - 2 * ne) + ne * i + ne]
+            if codes:
+                parts.append((rc, es, sem, u8(T, dstbuf, 0, w), u8(T, buf, w * i, w * i + w)))
+            else:
+                parts.append((rc, es, sem, T[dstbuf][:, 0:w], T[buf][:, w * i:w * i + w]))
+        fused([(buf, 0, 2 * w)], parts)
+
+    def to_near(buf, w, dstbuf, place, sem):
+        codes = SCRATCH[buf][2] == F8
+        parts = []
+        for k, d in enumerate(near):
+            if d == me:
+                continue
+            a, dc, n = place(d), T.cores[d], len(parts)
+            es = topo.engines(core, dc)[FN * n:FN * n + FN]
+            if codes:
+                parts.append((dc, es, sem, u8(T, dstbuf, a, a + w), u8(T, buf, w * k, w * k + w)))
+            else:
+                parts.append((dc, es, sem, T[dstbuf][:, a:a + w], T[buf][:, w * k:w * k + w]))
+        fused([(buf, 0, 4 * w)], parts)
+
+    for i in range(2):
+        k = pl["far"][i][0] // 2
+        pick("sf", 64 * i, "qx", 130, "offs", 4 * k, 4 * k + 4)
+    to_relays("sf", 64, "rz", "rzc", FF)
+    to_relays("sf_s", 64, "rz_s", "rzs", FF)
+    for i in range(2):
+        k = pl["near"][i][0] // 2
+        pick("sn", 64 * i, "qx", 130, "offs", 4 * k, 4 * k + 4)
+
+    def at_near(d):
+        p = plan(T, topo, T.cores[d])
+        return 32 * (p["near"][0] + p["near"][1]).index(me)
+    to_near("sn", 32, "zn", at_near, "azn")
+    to_near("sn_s", 32, "zn_s", at_near, "azn")
+
+    def keep(dst, d0, src, s0):
+        dma("y", u8(T, dst, d0, d0 + 32), u8(T, src, s0, s0 + 32), [(src, s0, s0 + 32)], [(dst, d0, d0 + 32)])
+        dma("y", T[dst + "_s"][:, d0:d0 + 32], T[src + "_s"][:, s0:s0 + 32], [(src + "_s", s0, s0 + 32)], [(dst + "_s", d0, d0 + 32)])
+    keep("zn", 32 * own, "sn", 32 * own)
+
+    vts(("mk", 0, 32), ("hp", 0, 32), HQ, None, OP.is_equal)
+    vts(("a2", 0, 32), ("la0", 0, 32), R16, None, OP.add)
+    vtt(("a3", 0, 32), ("a2", 0, 32), ("mk", 0, 32), OP.mult)
+    vts(("offd", 0, 32), ("a3", 0, 32), 128.0, None, OP.add)
+    vts(E0, U1, -1.0, 1.0, OP.mult, OP.add)
+    quant("qb1", 0, ("b1t", 0, 512))
+    quant("zn", 128, ("zt", 0, 512))
+    quant("zf", 128, ("zt", 0, 512))
+    vts(("gm", 0, 520), ("gp", 0, 520), -1.0, None, OP.mult)
+    for b in range(4):
+        quant("qe", 128 * b, ("gp", 3 - b, 515 - b))
+        quant("qm", 128 * b, ("gm", 3 - b, 515 - b))
+    quant("rqn", 128, ("zt", 0, 512))
+    quant("rqf", 128, ("zt", 0, 512))
+    quant("qb2", 0, ("b2t", 0, 512))
+    for x in ("n", "f", "h"):
+        vset(("xs" + x, 0, 32), 0.0)
+
+    def spread(x, i, out, plus):
+        s = "xs" + x
+        vts((s, 0, 8, 2), i, E0, None, OP.mult)
+        vts((s, 1, 8, 2), i, U1, None, OP.mult)
+        yield
+        vtr((s, 32, 64), (s, 0, 32))
+        yield
+        vtt((s, 64, 80), (s, 32, 48), (s, 48, 64), OP.add)
+        vtt((s, 80, 96), (s, 32, 48), (s, 48, 64), OP.add)
+        yield
+        vtr((s, 96, 128), (s, 64, 96))
+        yield
+        vts((out, 0, 8), (s, 96, 104), plus, None, OP.add)
+
+    vtt(MU, M0, E0, OP.mult)
+    vts(DC, D8, 32.0, -257.0, OP.mult, OP.add)
+    vts(("t1", 0, 128), ("inc", 0, 128), 32.5, MU, OP.is_le, OP.mult)
+    vts(("t3", 0, 128), ("inc", 0, 128), DC, None, OP.add)
+    vtt(("t2", 0, 128), ("t1", 0, 128), ("ohf", 0, 128), OP.mult)
+    vtt(("t4", 0, 128), ("t2", 0, 128), ("t3", 0, 128), OP.mult)
+    vtr(("t1", 0, 128), ("t4", 0, 128))
+    for b in range(4):
+        vsum(("sl", b, b + 1), ("t1", 32 * b, 32 * b + 32))
+    for _ in spread("h", ("sl", 0, 4), "offh", 256.0):
+        pass
+    quant("lv1", 256, ("zt", 0, 512))
+    quant("lv2", 256, ("zt", 0, 512))
+    quant("qw", 0, ("wt", 0, 512))
+    vset(("xw", 0, 512), 0.0)
+    vset(("xtw", 256, 288), -1.0)
+    vset(("xtw", 544, 576), -1.0)
+
+    def level(x, l):
+        win, book, dg, pm, nn, off = ("z" if l == 1 else "rq") + x, "qb%d" % l, "dg%d%s" % (l, x), "pm" + x, "nn" + x, "off%d%s" % (l, x)
+        turn = 2 if (x, l) == ("n", 2) else 0
+
+        def first(b):
+            pick(dg, 128 * b, win, 130, "offd", 8 * b, 8 * b + 8)
+            mm("sc", (b + turn) % 4, dg, 128 * b, book, 0)
+
+        def second(b):
+            p, k = (pm, 128 * b, 128 * b + 128), 512 * ((b + turn) % 4)
+            vscan(p, ("zt", 0, 128), ("sc", k, k + 128), BIG, OP.add, OP.max)
+            act(("jk", 128 * b, 128 * b + 128), p, AF.Sign, bias=(pm, 128 * b + 127, 128 * b + 128), scale=-1.0,
+                acc=(nn, 2 * b + l - 1, 2 * b + l))
+
+        def scores():
+            first(0)
+            first(1)
+            second(0)
+            first(2)
+            second(1)
+            first(3)
+            second(2)
+            second(3)
+
+        def words():
+            for _ in spread(x, (nn, l - 1, 8, 2), off, 0.0):
+                yield
+
+        def take():
+            pick("v%d%s" % (l, x), 0, book, 128, off, 0, 8)
+        return first, second, scores, words, take
+
+    def run(gen):
+        for _ in gen:
+            pass
+
+    def back(x, l):
+        v, lv = "v%d%s" % (l, x), "lv%d" % l
+        if x == "f":
+            to_relays(v, 64, "rv%d" % l, "r%dc" % l, FB)
+            to_relays(v + "_s", 64, "rv%d_s" % l, "r%ds" % l, FB)
+        else:
+            to_near(v, 32, lv, lambda d: 32 * me, "hv%dn" % l)
+            to_near(v + "_s", 32, lv + "_s", lambda d: 32 * me, "hv%dn" % l)
+            keep(lv, 32 * me, v, 32 * own)
+
+    n2first, n2second, _s, n2words, n2take = level("n", 2)
+    for x in ("n", "f"):
+        first, second, scores, words, take = level(x, 1)
+        scores()
+        for b in range(4):
+            mm("dd", b, "qe", 128 * b, "z" + x, 0, True, False)
+        run(words())
+        take()
+        back(x, 1)
+        rt = "rt" + x
+        for b in range(4):
+            mm("dd", b, "qm", 128 * b, "v1" + x, 0, False, True)
+        if x == "f":
+            pick_codes("dg2n", 0, "rqn", 130, "offd", 0, 8)
+        vcopy((rt, 0, 512, 4), ("dd", 0, 128))
+        act((rt, 1, 512, 4), ("dd", 512, 640), AF.Copy)
+        if x == "f":
+            pick_codes("dg2n", 128, "rqn", 130, "offd", 8, 16)
+        vcopy((rt, 2, 512, 4), ("dd", 1024, 1152))
+        act((rt, 3, 512, 4), ("dd", 1536, 1664), AF.Copy)
+        if x == "f":
+            pick_scales("dg2n", 0, "rqn", 130, "offd", 0, 8)
+        quant("rq" + x, 0, (rt, 0, 512))
+    first, second, scores, words, take = level("f", 2)
+    scores()
+    w = words()
+    fill = [lambda: n2first(2), lambda: n2first(3)]
+    pick_scales("dg2n", 128, "rqn", 130, "offd", 8, 16)
+    for b in range(2):
+        mm("sc", b + 2, "dg2n", 128 * b, "qb2", 0)
+    for _ in w:
+        if fill:
+            fill.pop(0)()
+    take()
+    to_relays("nnf", 4, "rn", "rnc", FB)
+    back("f", 2)
+    for b in range(4):
+        n2second(b)
+    run(n2words())
+    n2take()
+    to_near("nnn", 2, "lan", lambda d: 2 * me, "hnn")
+    dma("y", T.lan[:, 2 * me:2 * me + 2], T.nnn[:, 2 * own:2 * own + 2], [("nnn", 2 * own, 2 * own + 2)], [("lan", 2 * me, 2 * me + 2)])
+    back("n", 2)
+
+    def store(l):
+        h = "h%d" % l
+        o = 128 * (l - 1)
+        dma("y", T.oc[:, 4 * o:4 * o + 512], u8(T, h, 0, 128), [(h, 0, 128)], [], True)
+        for k in range(4):
+            dma("y" if k % 2 else "s", T.osc[4 * k:4 * k + 4, o:o + 128], T[h + "_s"][32 * k:32 * k + 4, 0:128], [(h + "_s", 0, 128)], [], True)
+
+    pick("h1", 0, "lv1", 258, "offh", 0, 8)
+    store(1)
+    mm("sc", 0, "qw", 0, "h1", 0, True, False)
+    for l in range(2):
+        vcopy(("xw", 256 * l, 256 * l + 256, 32), ("lan", l, 16, 2))
+    for l in range(2):
+        vtr(("xtw", 288 * l, 288 * l + 256), ("xw", 256 * l, 256 * l + 256))
+    for l in range(2):
+        o, w, f = ("wnt", 128 * l, 128 * l + 128), ("xtw", 288 * l, 288 * l + 288), ("offh", 0, 8)
+        op("v", lambda: g.vector.tensor_copy(ap(o), ap(w).indirect(ap(f))), [w, f], [o])
+        dma("y", T.wn[4 * l:4 * l + 4, :], T.wnt[0:128:32, 128 * l:128 * l + 128], [o], [], True)
+    pick("h2", 0, "lv2", 258, "offh", 0, 8)
+    mm("sc", 0, "qw", 0, "h2", 0, False, True)
+    op("v", lambda: g.vector.tensor_copy(ap(("yt", 0, 128)), ap(("sc", 0, 128))), [("sc", 0, 128)], [("yt", 0, 128)])
+    dma("s", T.y[:], T.yt[:], [("yt", 0, 128)], [], True)
+    store(2)
+    for s in total:
+        if waited.get(s, 0) < total[s]:
+            g.wait_ge(T.sem[s], total[s])

@@ -29,7 +29,7 @@ for _n, _w in (("xt", 512), ("ct", 512), ("b1t", 512), ("b2t", 512), ("wt", 512)
 for _n, _w in (("rst", 128), ("ts", 128), ("pm0", 128), ("pmn", 512), ("pmf", 512), ("cf", 32), ("kb0", 8), ("kb", 8),
                ("la0", 32), ("hp", 32), ("mk", 32), ("a2", 32), ("a3", 32), ("cnt", 8), ("x0", 32), ("xt0", 32), ("y0", 16),
                ("t1", 128), ("t2", 128), ("t3", 128), ("t4", 128), ("sl", 4),
-               ("nnn", 8), ("nnf", 8), ("rn", 4), ("lan", 16), ("wnt", 256), ("yt", 128),
+               ("nnn", 8), ("nnf", 8), ("rn", 4), ("rp", 2), ("lan", 16), ("wnt", 256), ("yt", 128),
                ("xsn", 128), ("xsf", 128), ("xsh", 128)):
     _buf(_n, _w)
 _buf("ip", 1, "int32")
@@ -41,17 +41,21 @@ SCRATCH["dd"] = ("psum", [128, 2048], "float32")
 
 SEMAPHORES = (["ev", "es", "et", "ep", "sent", "st"] + ["l%d" % i for i in range(20)]
               + ["azn", "azf", "hv1n", "hv1f", "hv2n", "hv2f", "hnn", "hnf"]
-              + ["rzc", "rzs", "r1c", "r1s", "rnc", "r2c", "r2s"])
+              + ["rzc", "rzs", "r1c", "r1s", "rnc", "r2c", "r2s", "rpn"])
 
 VS = 5
 FN = 4
+FM = 8
 FF = 4
-FB = 8
 FR = 4
+FP = 8
 BIG = -9e29
+PLANS = {}
 
 
 def plan(T, topo, core):
+    if core in PLANS:
+        return PLANS[core]
     cs = list(T.cores)
     here = [c for c in cs if c in topo.cores_of(core)]
     plane = [c for c in cs if c not in here and topo.same_plane(core, c)]
@@ -60,9 +64,16 @@ def plan(T, topo, core):
     g1 = [c for c in far if c not in g0]
     rel = [c for c in topo.cores_of(core) if c not in cs and topo.die(c) == topo.die(core)
            and all(topo.may_write(c, d) for d in far)]
+    srel = []
+    for grp in (g0, g1):
+        cand = [c for c in range(256) if topo.mates(c, grp[0]) and topo.die(c) == topo.die(core) and topo.same_plane(core, c)
+                and all(topo.may_write(c, d) for d in grp)]
+        users = [c for c in cs if topo.same_plane(c, cand[0]) and topo.die(c) == topo.die(core)]
+        srel.append(cand[users.index(core)])
     rk = T.rank_of
-    return {"near": [[rk(c) for c in plane], [rk(c) for c in here]], "far": [[rk(c) for c in g0], [rk(c) for c in g1]],
-            "relays": rel[:2]}
+    PLANS[core] = {"near": [[rk(c) for c in plane], [rk(c) for c in here]], "far": [[rk(c) for c in g0], [rk(c) for c in g1]],
+                   "codes": rel[:2], "scales": srel}
+    return PLANS[core]
 
 
 def bits(es):
@@ -89,20 +100,20 @@ def u8(T, name, a, b):
 
 
 def relay_program(g, core, T, topo):
-    src, grp = None, None
+    src, grp, role, to = None, None, None, None
     for c in T.cores:
-        if c in topo.cores_of(core):
-            p = plan(T, topo, c)
-            for i in range(2):
-                if p["relays"][i] == core:
-                    src, grp = T.rank_of(c), p["far"][i]
+        p = plan(T, topo, c)
+        for i in range(2):
+            for k in ("codes", "scales"):
+                if p[k][i] == core:
+                    src, grp, role, to = T.rank_of(c), p["far"][i], k, p["near"][0][i]
     if src is None:
         return
     sent = [0]
 
-    def hand(wait, n, sem, mk):
+    def hand(wait, sem, mk):
         ts = []
-        g.wait_ge(T.sem[wait], n)
+        g.wait_ge(T.sem[wait], FF)
         for j, d in enumerate(grp):
             dst = T.cores[d]
             es = topo.engines(core, dst)[FR * j:FR * j + FR]
@@ -113,14 +124,21 @@ def relay_program(g, core, T, topo):
             sent[0] += FR
         g.remote_dma_fused(ts, local_sem=T.sem.sent)
 
-    hand("rzc", FF, "azf", lambda j, at: (u8(T, "zf", 32 * at, 32 * at + 32), u8(T, "rz", 32 * j, 32 * j + 32)))
-    hand("rzs", FF, "azf", lambda j, at: (T["zf_s"][:, 32 * at:32 * at + 32], T["rz_s"][:, 32 * j:32 * j + 32]))
     o = 32 * src
-    hand("r1c", FB, "hv1f", lambda j, at: (u8(T, "lv1", o, o + 32), u8(T, "rv1", 32 * j, 32 * j + 32)))
-    hand("r1s", FB, "hv1f", lambda j, at: (T["lv1_s"][:, o:o + 32], T["rv1_s"][:, 32 * j:32 * j + 32]))
-    hand("rnc", FB, "hnf", lambda j, at: (T["lan"][:, 2 * src:2 * src + 2], T["rn"][:, 2 * j:2 * j + 2]))
-    hand("r2c", FB, "hv2f", lambda j, at: (u8(T, "lv2", o, o + 32), u8(T, "rv2", 32 * j, 32 * j + 32)))
-    hand("r2s", FB, "hv2f", lambda j, at: (T["lv2_s"][:, o:o + 32], T["rv2_s"][:, 32 * j:32 * j + 32]))
+    if role == "codes":
+        hand("rzc", "azf", lambda j, at: (u8(T, "zf", 32 * at, 32 * at + 32), u8(T, "rz", 32 * j, 32 * j + 32)))
+        hand("r1c", "hv1f", lambda j, at: (u8(T, "lv1", o, o + 32), u8(T, "rv1", 32 * j, 32 * j + 32)))
+        hand("r2c", "hv2f", lambda j, at: (u8(T, "lv2", o, o + 32), u8(T, "rv2", 32 * j, 32 * j + 32)))
+        g.wait_ge(T.sem.rpn, FF)
+        dst = T.cores[to]
+        es = topo.engines(core, dst)[:FP]
+        g.remote_dma_fused([xfer(T, topo, core, dst, es, "hnn", T["lan"][:, 2 * src:2 * src + 2], T["rp"][:, 0:2])], local_sem=T.sem.sent)
+        sent[0] += FP
+    else:
+        hand("rzs", "azf", lambda j, at: (T["zf_s"][:, 32 * at:32 * at + 32], T["rz_s"][:, 32 * j:32 * j + 32]))
+        hand("r1s", "hv1f", lambda j, at: (T["lv1_s"][:, o:o + 32], T["rv1_s"][:, 32 * j:32 * j + 32]))
+        hand("rnc", "hnf", lambda j, at: (T["lan"][:, 2 * src:2 * src + 2], T["rn"][:, 2 * j:2 * j + 2]))
+        hand("r2s", "hv2f", lambda j, at: (T["lv2_s"][:, o:o + 32], T["rv2_s"][:, 32 * j:32 * j + 32]))
     g.wait_ge(T.sem.sent, sent[0])
 
 
@@ -298,10 +316,11 @@ def home_program(g, core, T, topo):
             hw1 += both("lv1", 32 * r, 32 * r + 32)
             hw2 += both("lv2", 32 * r, 32 * r + 32)
             nn_.append(("lan", 2 * r, 2 * r + 2))
-    arrive("azn", 3 * 2 * FN, nw)
-    arrive("hv1n", 3 * 2 * FN, hw1)
-    arrive("hv2n", 3 * 2 * FN, hw2)
-    arrive("hnn", 3 * FN, nn_)
+    from_near = 2 * FN + FM
+    arrive("azn", 2 * from_near, nw)
+    arrive("hv1n", 2 * from_near, hw1)
+    arrive("hv2n", 2 * from_near, hw2)
+    arrive("hnn", 2 * FP + FM, nn_)
     arrive("azf", 4 * 2 * FR, both("zf", 0, 128))
     hw1, hw2, nn_ = [], [], []
     for r in far:
@@ -341,14 +360,16 @@ def home_program(g, core, T, topo):
     R16, HQ, D8, U0, U1, VV = [C(k) for k in range(6)]
     M0, E0, KC, AL, BE, T0, MU, DC = [C(k) for k in range(8, 16)]
     vts(("oco", 0, 8), ("zt", 0, 8), D8, None, OP.add)
-    quant("qc", 0, ("ct", 0, 512))
-    pick("qr", 0, "qc", 128, "oco", 0, 8)
     vset(("rst", 0, 128), 0.0)
     vset(("rst", 0, 128, 8), BIG)
     vts(M0, U0, -1.0, 1.0, OP.mult, OP.add)
     vts(T0, U1, 16.0, 0.5, OP.mult, OP.add)
     vtt(KC, T0, U0, OP.add)
     vts(("kb", 0, 8), ("kb0", 0, 8), KC, None, OP.add)
+    vts(BE, VV, float(VS), 64.0, OP.is_lt, OP.mult)
+    vts(AL, BE, -1.0 / 128, 1.0, OP.mult, OP.add)
+    quant("qc", 0, ("ct", 0, 512))
+    pick("qr", 0, "qc", 128, "oco", 0, 8)
 
     quant("qx", 0, ("xt", 0, 512))
     mm("sc", 0, "qr", 0, "qx", 0)
@@ -368,8 +389,6 @@ def home_program(g, core, T, topo):
         vts(c, ("inc", 0, 128), ("kb", v, v + 1), None, OP.is_le)
     for v in range(VS, 8):
         vsum(("cnt", v, v + 1), ("cmp", 128 * (v - VS), 128 * (v - VS) + 128))
-    vts(BE, VV, float(VS), 64.0, OP.is_lt, OP.mult)
-    vts(AL, BE, -1.0 / 128, 1.0, OP.mult, OP.add)
     for e in range(2):
         act(("x0", 16 * e + 1, 16 * e + 16, 2), ("cnt", 0, 8), AF.Copy, scale=U0)
         vts(("x0", 16 * e, 16 * e + 16, 2), ("cnt", 0, 8), M0, None, OP.mult)
@@ -378,25 +397,27 @@ def home_program(g, core, T, topo):
         vtt(("y0", u, 16, 2), ("xt0", 16 * u, 16 * u + 8), ("xt0", 16 * u + 8, 16 * u + 16), OP.add)
     vts(("offs", 0, 16), ("y0", 0, 16), AL, BE, OP.mult, OP.add)
 
-    def to_relays(buf, w, dstbuf, sem, ne):
+    def to_relays(kind, buf, w, dstbuf, sem):
         codes = SCRATCH[buf][2] == F8
         parts = []
-        for i, rc in enumerate(pl["relays"]):
-            es = topo.engines(core, rc)[(16 - 2 * ne) + ne * i:(16 - 2 * ne) + ne * i + ne]
+        for i, rc in enumerate(pl[kind]):
+            es = topo.engines(core, rc)
+            k = (len(es) - 2 * FF) + FF * i
             if codes:
-                parts.append((rc, es, sem, u8(T, dstbuf, 0, w), u8(T, buf, w * i, w * i + w)))
+                parts.append((rc, es[k:k + FF], sem, u8(T, dstbuf, 0, w), u8(T, buf, w * i, w * i + w)))
             else:
-                parts.append((rc, es, sem, T[dstbuf][:, 0:w], T[buf][:, w * i:w * i + w]))
+                parts.append((rc, es[k:k + FF], sem, T[dstbuf][:, 0:w], T[buf][:, w * i:w * i + w]))
         fused([(buf, 0, 2 * w)], parts)
 
-    def to_near(buf, w, dstbuf, place, sem):
+    def to_near(buf, w, dstbuf, place, sem, some):
         codes = SCRATCH[buf][2] == F8
         parts = []
         for k, d in enumerate(near):
-            if d == me:
+            if d == me or d not in some:
                 continue
             a, dc, n = place(d), T.cores[d], len(parts)
-            es = topo.engines(core, dc)[FN * n:FN * n + FN]
+            es = topo.engines(core, dc)
+            es = es[len(es) - FM:] if d in pl["near"][1] else es[FN * n:FN * n + FN]
             if codes:
                 parts.append((dc, es, sem, u8(T, dstbuf, a, a + w), u8(T, buf, w * k, w * k + w)))
             else:
@@ -406,8 +427,8 @@ def home_program(g, core, T, topo):
     for i in range(2):
         k = pl["far"][i][0] // 2
         pick("sf", 64 * i, "qx", 130, "offs", 4 * k, 4 * k + 4)
-    to_relays("sf", 64, "rz", "rzc", FF)
-    to_relays("sf_s", 64, "rz_s", "rzs", FF)
+    to_relays("codes", "sf", 64, "rz", "rzc")
+    to_relays("scales", "sf_s", 64, "rz_s", "rzs")
     for i in range(2):
         k = pl["near"][i][0] // 2
         pick("sn", 64 * i, "qx", 130, "offs", 4 * k, 4 * k + 4)
@@ -415,8 +436,8 @@ def home_program(g, core, T, topo):
     def at_near(d):
         p = plan(T, topo, T.cores[d])
         return 32 * (p["near"][0] + p["near"][1]).index(me)
-    to_near("sn", 32, "zn", at_near, "azn")
-    to_near("sn_s", 32, "zn_s", at_near, "azn")
+    to_near("sn", 32, "zn", at_near, "azn", near)
+    to_near("sn_s", 32, "zn_s", at_near, "azn", near)
 
     def keep(dst, d0, src, s0):
         dma("y", u8(T, dst, d0, d0 + 32), u8(T, src, s0, s0 + 32), [(src, s0, s0 + 32)], [(dst, d0, d0 + 32)])
@@ -443,8 +464,8 @@ def home_program(g, core, T, topo):
 
     def spread(x, i, out, plus):
         s = "xs" + x
-        vts((s, 0, 8, 2), i, E0, None, OP.mult)
-        vts((s, 1, 8, 2), i, U1, None, OP.mult)
+        act((s, 0, 8, 2), i, AF.Copy, scale=E0)
+        act((s, 1, 8, 2), i, AF.Copy, scale=U1)
         yield
         vtr((s, 32, 64), (s, 0, 32))
         yield
@@ -477,25 +498,21 @@ def home_program(g, core, T, topo):
         win, book, dg, pm, nn, off = ("z" if l == 1 else "rq") + x, "qb%d" % l, "dg%d%s" % (l, x), "pm" + x, "nn" + x, "off%d%s" % (l, x)
         turn = 2 if (x, l) == ("n", 2) else 0
 
-        def first(b):
-            pick(dg, 128 * b, win, 130, "offd", 8 * b, 8 * b + 8)
-            mm("sc", (b + turn) % 4, dg, 128 * b, book, 0)
+        def codes(p):
+            pick_codes(dg, 256 * p, win, 130, "offd", 16 * p, 16 * p + 16)
 
-        def second(b):
+        def scales(p):
+            pick_scales(dg, 256 * p, win, 130, "offd", 16 * p, 16 * p + 16)
+
+        def score(p):
+            for b in range(2 * p, 2 * p + 2):
+                mm("sc", (b + turn) % 4, dg, 128 * b, book, 0)
+
+        def best(b):
             p, k = (pm, 128 * b, 128 * b + 128), 512 * ((b + turn) % 4)
             vscan(p, ("zt", 0, 128), ("sc", k, k + 128), BIG, OP.add, OP.max)
             act(("jk", 128 * b, 128 * b + 128), p, AF.Sign, bias=(pm, 128 * b + 127, 128 * b + 128), scale=-1.0,
                 acc=(nn, 2 * b + l - 1, 2 * b + l))
-
-        def scores():
-            first(0)
-            first(1)
-            second(0)
-            first(2)
-            second(1)
-            first(3)
-            second(2)
-            second(3)
 
         def words():
             for _ in spread(x, (nn, l - 1, 8, 2), off, 0.0):
@@ -503,7 +520,7 @@ def home_program(g, core, T, topo):
 
         def take():
             pick("v%d%s" % (l, x), 0, book, 128, off, 0, 8)
-        return first, second, scores, words, take
+        return codes, scales, score, best, words, take
 
     def run(gen):
         for _ in gen:
@@ -512,17 +529,22 @@ def home_program(g, core, T, topo):
     def back(x, l):
         v, lv = "v%d%s" % (l, x), "lv%d" % l
         if x == "f":
-            to_relays(v, 64, "rv%d" % l, "r%dc" % l, FB)
-            to_relays(v + "_s", 64, "rv%d_s" % l, "r%ds" % l, FB)
+            to_relays("codes", v, 64, "rv%d" % l, "r%dc" % l)
+            to_relays("scales", v + "_s", 64, "rv%d_s" % l, "r%ds" % l)
         else:
-            to_near(v, 32, lv, lambda d: 32 * me, "hv%dn" % l)
-            to_near(v + "_s", 32, lv + "_s", lambda d: 32 * me, "hv%dn" % l)
+            to_near(v, 32, lv, lambda d: 32 * me, "hv%dn" % l, near)
+            to_near(v + "_s", 32, lv + "_s", lambda d: 32 * me, "hv%dn" % l, near)
             keep(lv, 32 * me, v, 32 * own)
 
-    n2first, n2second, _s, n2words, n2take = level("n", 2)
+    n2codes, n2scales, n2score, n2best, n2words, n2take = level("n", 2)
     for x in ("n", "f"):
-        first, second, scores, words, take = level(x, 1)
-        scores()
+        codes, scales, score, best, words, take = level(x, 1)
+        for p in range(2):
+            codes(p)
+            scales(p)
+            score(p)
+        for b in range(4):
+            best(b)
         for b in range(4):
             mm("dd", b, "qe", 128 * b, "z" + x, 0, True, False)
         run(words())
@@ -532,36 +554,38 @@ def home_program(g, core, T, topo):
         for b in range(4):
             mm("dd", b, "qm", 128 * b, "v1" + x, 0, False, True)
         if x == "f":
-            pick_codes("dg2n", 0, "rqn", 130, "offd", 0, 8)
+            n2codes(0)
         vcopy((rt, 0, 512, 4), ("dd", 0, 128))
         act((rt, 1, 512, 4), ("dd", 512, 640), AF.Copy)
-        if x == "f":
-            pick_codes("dg2n", 128, "rqn", 130, "offd", 8, 16)
         vcopy((rt, 2, 512, 4), ("dd", 1024, 1152))
         act((rt, 3, 512, 4), ("dd", 1536, 1664), AF.Copy)
         if x == "f":
-            pick_scales("dg2n", 0, "rqn", 130, "offd", 0, 8)
+            n2scales(0)
         quant("rq" + x, 0, (rt, 0, 512))
-    first, second, scores, words, take = level("f", 2)
-    scores()
-    w = words()
-    fill = [lambda: n2first(2), lambda: n2first(3)]
-    pick_scales("dg2n", 128, "rqn", 130, "offd", 8, 16)
-    for b in range(2):
-        mm("sc", b + 2, "dg2n", 128 * b, "qb2", 0)
-    for _ in w:
-        if fill:
-            fill.pop(0)()
+    codes, scales, score, best, words, take = level("f", 2)
+    for p in range(2):
+        codes(p)
+        scales(p)
+        score(p)
+    for b in range(4):
+        best(b)
+    n2score(0)
+    for k, _ in enumerate(words()):
+        if k == 0:
+            n2codes(1)
+            n2scales(1)
+            n2score(1)
     take()
-    to_relays("nnf", 4, "rn", "rnc", FB)
+    to_relays("scales", "nnf", 4, "rn", "rnc")
     back("f", 2)
     for b in range(4):
-        n2second(b)
+        n2best(b)
     run(n2words())
     n2take()
-    to_near("nnn", 2, "lan", lambda d: 2 * me, "hnn")
     dma("y", T.lan[:, 2 * me:2 * me + 2], T.nnn[:, 2 * own:2 * own + 2], [("nnn", 2 * own, 2 * own + 2)], [("lan", 2 * me, 2 * me + 2)])
+    to_relays("codes", "nnn", 2, "rp", "rpn")
     back("n", 2)
+    to_near("nnn", 2, "lan", lambda d: 2 * me, "hnn", pl["near"][1])
 
     def store(l):
         h = "h%d" % l
@@ -573,19 +597,21 @@ def home_program(g, core, T, topo):
     pick("h1", 0, "lv1", 258, "offh", 0, 8)
     store(1)
     mm("sc", 0, "qw", 0, "h1", 0, True, False)
+    pick("h2", 0, "lv2", 258, "offh", 0, 8)
+    mm("sc", 0, "qw", 0, "h2", 0, False, True)
+    store(2)
     for l in range(2):
         vcopy(("xw", 256 * l, 256 * l + 256, 32), ("lan", l, 16, 2))
     for l in range(2):
         vtr(("xtw", 288 * l, 288 * l + 256), ("xw", 256 * l, 256 * l + 256))
-    for l in range(2):
-        o, w, f = ("wnt", 128 * l, 128 * l + 128), ("xtw", 288 * l, 288 * l + 288), ("offh", 0, 8)
-        op("v", lambda: g.vector.tensor_copy(ap(o), ap(w).indirect(ap(f))), [w, f], [o])
-        dma("y", T.wn[4 * l:4 * l + 4, :], T.wnt[0:128:32, 128 * l:128 * l + 128], [o], [], True)
-    pick("h2", 0, "lv2", 258, "offh", 0, 8)
-    mm("sc", 0, "qw", 0, "h2", 0, False, True)
-    op("v", lambda: g.vector.tensor_copy(ap(("yt", 0, 128)), ap(("sc", 0, 128))), [("sc", 0, 128)], [("yt", 0, 128)])
+    act(("yt", 0, 128), ("sc", 0, 128), AF.Copy)
     dma("s", T.y[:], T.yt[:], [("yt", 0, 128)], [], True)
-    store(2)
+    o, w, f = ("wnt", 0, 128), ("xtw", 0, 288), ("offh", 0, 8)
+    op("v", lambda: g.vector.tensor_copy(ap(o), ap(w).indirect(ap(f))), [w, f], [o])
+    dma("y", T.wn[0:4, :], T.wnt[0:128:32, 0:128], [o], [], True)
+    o2, w2 = ("wnt", 128, 256), ("xtw", 288, 576)
+    op("s", lambda: g.scalar.activation(ap(o2), ap(w2).indirect(ap(f)), AF.Copy), [w2, f], [o2])
+    dma("s", T.wn[4:8, :], T.wnt[0:128:32, 128:256], [o2], [], True)
     for s in total:
         if waited.get(s, 0) < total[s]:
             g.wait_ge(T.sem[s], total[s])

@@ -17,40 +17,45 @@ def _buf(name, n, ty="float32"):
     SCRATCH[name] = ("sbuf", [128, n], ty)
 
 
-for _n, _w in (("qx", 256), ("qc", 128), ("qr", 128), ("qb1", 128), ("qb2", 128), ("qw", 128), ("qe", 512), ("qm", 512),
-               ("sf", 128), ("sn", 128), ("zn", 256), ("zf", 256), ("dg1n", 512), ("dg1f", 512), ("dg2n", 512), ("dg2f", 512),
-               ("v1n", 128), ("v1f", 128), ("v2n", 128), ("v2f", 128), ("rqn", 256), ("rqf", 256),
+for _n, _w in (("qx", 130), ("qc", 128), ("qo", 128), ("qtri", 128), ("qs", 144), ("qw16", 128), ("qln", 136), ("qlf", 136),
+               ("qb1", 512), ("qb2", 512), ("qw", 128), ("qe", 512), ("qm", 512),
+               ("sf", 128), ("sn", 128), ("zn", 128), ("zf", 128),
+               ("v1n", 128), ("v1f", 128), ("v2n", 128), ("v2f", 128), ("rqn", 128), ("rqf", 128),
                ("lv1", 384), ("lv2", 384), ("h1", 128), ("h2", 128), ("rz", 64), ("rv1", 64), ("rv2", 64)):
     _codes(_n, _w)
-for _n, _w in (("xt", 512), ("ct", 512), ("b1t", 512), ("b2t", 512), ("wt", 512), ("zt", 512), ("onb", 520), ("gp", 520), ("gm", 520),
-               ("le", 128), ("oh", 128), ("ohf", 128), ("inc", 128), ("cmp", 384), ("jk", 512), ("rtn", 512), ("rtf", 512),
-               ("xw", 512), ("xtw", 576)):
+for _n, _w in (("xt", 520), ("zr", 512), ("zb", 544), ("xb", 608), ("sx", 576), ("b1t", 2048), ("b2t", 2048), ("wt", 512), ("onb", 520),
+               ("gp", 520), ("gm", 520), ("tri", 512), ("w16", 512), ("ir", 128), ("itr", 128), ("ik", 128), ("imx", 64), ("mxx", 64),
+               ("ict", 16), ("rst", 256), ("jk", 512), ("rtn", 512), ("rtf", 512), ("xw", 256), ("xtw", 288)):
     _buf(_n, _w, "bfloat16")
-for _n, _w in (("rst", 128), ("ts", 128), ("pm0", 128), ("pmn", 512), ("pmf", 512), ("cf", 32), ("kb0", 8), ("kb", 8),
-               ("la0", 32), ("hp", 32), ("mk", 32), ("a2", 32), ("a3", 32), ("cnt", 8), ("x0", 32), ("xt0", 32), ("y0", 16),
-               ("t1", 128), ("t2", 128), ("t3", 128), ("t4", 128), ("sl", 4),
-               ("nnn", 8), ("nnf", 8), ("rn", 4), ("rp", 2), ("lan", 16), ("wnt", 256), ("yt", 128),
-               ("xsn", 128), ("xsf", 128), ("xsh", 128)):
+for _n, _w in (("pmn", 512), ("pmf", 512), ("cf", 32), ("c256", 8), ("ioc", 4), ("tok", 1), ("pmc", 8), ("le", 16), ("g8", 8),
+               ("n4n", 4), ("n4f", 4), ("n4h", 4), ("hln", 8), ("hlf", 8), ("zt", 16), ("san", 8), ("saf", 8),
+               ("nnn", 8), ("nnf", 8), ("rn", 4), ("rp", 2), ("lan", 16), ("wnt", 128), ("yt", 128)):
     _buf(_n, _w)
 _buf("ip", 1, "int32")
 _buf("ic", 8, "int32")
-for _n, _w in (("oco", 8), ("offd", 32), ("offs", 16), ("offh", 8), ("off1n", 8), ("off1f", 8), ("off2n", 8), ("off2f", 8)):
+for _n, _w in (("offc", 4), ("offs", 16), ("offh", 8), ("off1n", 8), ("off1f", 8), ("off2n", 8), ("off2f", 8)):
     _buf(_n, _w, "uint16")
 SCRATCH["sc"] = ("psum", [128, 2048], "float32")
 SCRATCH["dd"] = ("psum", [128, 2048], "float32")
 
-SEMAPHORES = (["ev", "es", "et", "ep", "sent", "st"] + ["l%d" % i for i in range(20)]
+SEMAPHORES = (["ev", "es", "et", "ep", "sent", "st"] + ["l%d" % i for i in range(40)]
               + ["azn", "azf", "hv1n", "hv1f", "hv2n", "hv2f", "hnn", "hnf"]
               + ["rzc", "rzs", "r1c", "r1s", "rnc", "r2c", "r2s", "rpn"])
 
-VS = 5
+CAPP = 32
 FN = 4
 FM = 8
 FF = 4
 FR = 4
 FP = 8
 BIG = -9e29
+M16, M32, M256 = 1.5 * 2.0 ** 27, 1.5 * 2.0 ** 28, 1.5 * 2.0 ** 31
 PLANS = {}
+ORDER = """
+hl qb1 qe N1.score N1.scan0 N1.count0 N1.scan1 N1.count1 n.given N1.place qm F1.score N1.take n.minus F1.scan0 qb2 F1.count0
+n.rest F1.scan1 N1.number f.given F1.count1 n.repack N2.score F1.place N2.scan0 N2.count0 N2.scan1 F1.take N2.count1 f.minus
+N2.place f.rest N1.back f.repack F1.number N2.take F2.score F2.scan0 F1.back F2.count0 F2.scan1 F2.count1 F2.place N2.number
+N2.back F2.take F2.back qw F2.number f.nums n.nums1 n.nums2 fin"""
 
 
 def plan(T, topo, core):
@@ -137,8 +142,8 @@ def relay_program(g, core, T, topo):
     else:
         hand("rzs", "azf", lambda j, at: (T["zf_s"][:, 32 * at:32 * at + 32], T["rz_s"][:, 32 * j:32 * j + 32]))
         hand("r1s", "hv1f", lambda j, at: (T["lv1_s"][:, o:o + 32], T["rv1_s"][:, 32 * j:32 * j + 32]))
-        hand("rnc", "hnf", lambda j, at: (T["lan"][:, 2 * src:2 * src + 2], T["rn"][:, 2 * j:2 * j + 2]))
         hand("r2s", "hv2f", lambda j, at: (T["lv2_s"][:, o:o + 32], T["rv2_s"][:, 32 * j:32 * j + 32]))
+        hand("rnc", "hnf", lambda j, at: (T["lan"][:, 2 * src:2 * src + 2], T["rn"][:, 2 * j:2 * j + 2]))
     g.wait_ge(T.sem.sent, sent[0])
 
 
@@ -292,16 +297,20 @@ def home_program(g, core, T, topo):
         pick_codes(*a)
         pick_scales(*a)
 
-    def mm(ps, bank, l, l0, r, r0, start=True, stop=True):
-        o = (ps, 512 * bank, 512 * bank + 128)
-        a, sa, b, sb = (l, l0, l0 + 128), (l + "_s", l0, l0 + 128), (r, r0, r0 + 128), (r + "_s", r0, r0 + 128)
+    def mm(ps, bank, l, l0, r, r0, start=True, stop=True, n=128):
+        o = (ps, 512 * bank, 512 * bank + n)
+        a, sa, b, sb = (l, l0, l0 + 128), (l + "_s", l0, l0 + 128), (r, r0, r0 + n), (r + "_s", r0, r0 + n)
         op("t", lambda: g.tensor.matmul_mx(ap(o), ap(a), ap(sa), ap(b), ap(sb), start, stop), [a, sa, b, sb], [(ps, 512 * bank, 512 * bank + 512)])
 
-    dma("y", T.xt[:], T.x[:], [], [("xt", 0, 512)])
-    dma("s", T.ct[:, 0:32], T.co[:, 0:32], [], [("ct", 0, 32)])
-    dma("y", T.b1t[:], T.b1[:], [], [("b1t", 0, 512)])
-    dma("y", T.b2t[:], T.b2[:], [], [("b2t", 0, 512)])
+    dma("y", T.xt[:, 0:512], T.x[:], [], [("xt", 0, 512)])
+    dma("s", T.zb[:, 0:32], T.co[:, 0:32], [], [("zb", 0, 32)])
     dma("y", T.wt[:], T.w[:], [], [("wt", 0, 512)])
+
+    def book(b):
+        for h in range(4):
+            act((b + "t", 512 * h, 512 * h + 512), ("zr", 0, 512), AF.Copy)
+        for h in range(4):
+            dma("y", T[b + "t"][32 * h:32 * h + 32, 512 * h:512 * h + 512], T[b][32 * h:32 * h + 32, :], [], [(b + "t", 512 * h, 512 * h + 512)])
 
     near, far = pl["near"][0] + pl["near"][1], pl["far"][0] + pl["far"][1]
     own = near.index(me)
@@ -337,65 +346,67 @@ def home_program(g, core, T, topo):
         else:
             op("p", lambda: g.iota(ap(o), pat, base, cm, allow_small_or_imprecise_dtypes=True), [], [o])
 
-    iota(("ip", 0, 1), [[1, 1]], 0, 1)
-    iota(("kb0", 0, 8), [[2, 8]], 0, 0)
-    iota(("onb", 0, 520), [[0, 520]], 1, 0)
-    iota(("la0", 0, 32), [[32, 4], [0, 4], [16, 2]], -128, 0)
-    iota(("hp", 0, 32), [[0, 4], [1, 4], [0, 2]], 0, 0)
-    op("p", lambda: g.affine_select(T.gp[:, 0:520], T.onb[:, 0:520], [[-1, 520]], OP.is_equal, 0.0, 3, 4),
-       [("onb", 0, 520)], [("gp", 0, 520)])
-    vset(("ct", 32, 512), 0.0)
-    P1 = ("ip", 0, 1)
-    for k, (sh, m) in enumerate(((0, 15), (5, 7), (0, 7), (3, 1), (4, 1), (1, 7))):
-        o = ("ic", k, k + 1)
-        if sh:
-            vts(o, P1, sh, m, OP.arith_shift_right, OP.bitwise_and)
-        else:
-            vts(o, P1, m, None, OP.bitwise_and)
-    vset(("zt", 0, 512), 0.0)
-    vcopy(("cf", 0, 6), ("ic", 0, 6))
-
     def C(k):
         return ("cf", k, k + 1)
-    R16, HQ, D8, U0, U1, VV = [C(k) for k in range(6)]
-    M0, E0, KC, AL, BE, T0, MU, DC = [C(k) for k in range(8, 16)]
-    vts(("oco", 0, 8), ("zt", 0, 8), D8, None, OP.add)
-    vset(("rst", 0, 128), 0.0)
-    vset(("rst", 0, 128, 8), BIG)
-    vts(M0, U0, -1.0, 1.0, OP.mult, OP.add)
-    vts(T0, U1, 16.0, 0.5, OP.mult, OP.add)
-    vtt(KC, T0, U0, OP.add)
-    vts(("kb", 0, 8), ("kb0", 0, 8), KC, None, OP.add)
-    vts(BE, VV, float(VS), 64.0, OP.is_lt, OP.mult)
-    vts(AL, BE, -1.0 / 128, 1.0, OP.mult, OP.add)
-    quant("qc", 0, ("ct", 0, 512))
-    pick("qr", 0, "qc", 128, "oco", 0, 8)
+    R16, HQ, U1, P16, P3, E0, HQ128, CHI, CLO, G, FH, T0, T1, T2, T3, T4, T5 = [C(k) for k in range(17)]
+    TOK = ("tok", 0, 1)
+    pf = [q[0] // 2 for q in pl["far"]]
+    pn = [q[0] // 2 for q in pl["near"]]
+    iota(("c256", 0, 8), [[256, 8]], 0, 0)
+    iota(TOK, [[0, 1]], 0, 1)
+    iota(("itr", 0, 128), [[1, 128]], 0, 0)
+    iota(("ir", 0, 128), [[0, 8], [2, 16]], -15, 0)
+    iota(("ict", 0, 8), [[512 * (pf[1] - pf[0]), 2], [256, 2], [32, 2]], 512 * pf[0], 0)
+    iota(("ict", 8, 16), [[512 * (pn[1] - pn[0]), 2], [256, 2], [32, 2]], 512 * pn[0], 0)
+    iota(("ip", 0, 1), [[1, 1]], 0, 1)
+    iota(("ik", 0, 128), [[0, 2], [1, 16], [64, 4]], 0, 0)
+    iota(("imx", 0, 64), [[0, 2], [1, 8], [0, 4]], 0, 0)
+    iota(("ioc", 0, 4), [[4, 2], [0, 2]], 0, 0)
 
-    quant("qx", 0, ("xt", 0, 512))
-    mm("sc", 0, "qr", 0, "qx", 0)
-    quant("qx", 128, ("zt", 0, 512))
-    vtr(("ts", 0, 128), ("sc", 0, 128))
-    vscan(("pm0", 0, 128), ("rst", 0, 128), ("ts", 0, 128), 0.0, OP.add, OP.max)
-    for b in range(4):
-        vts(("le", 32 * b, 32 * b + 32), ("pm0", 32 * b, 32 * b + 32), ("pm0", 32 * b + 7, 32 * b + 8), None, OP.is_ge)
-    vtt(("oh", 1, 128), ("le", 1, 128), ("le", 0, 127), OP.subtract)
-    vcopy(("oh", 0, 128, 8), ("le", 0, 128, 8))
-    vtr(("ohf", 0, 128), ("oh", 0, 128))
-    vscan(("inc", 0, 128), ("onb", 0, 128), ("ohf", 0, 128), 0.0, OP.mult, OP.add)
-    for v in range(VS):
-        act(("jk", 128 * (v % 4), 128 * (v % 4) + 128), ("inc", 0, 128), AF.Sign, bias=("kb", v, v + 1), scale=-1.0, acc=("cnt", v, v + 1))
-    for v in range(VS, 8):
-        c = ("cmp", 128 * (v - VS), 128 * (v - VS) + 128)
-        vts(c, ("inc", 0, 128), ("kb", v, v + 1), None, OP.is_le)
-    for v in range(VS, 8):
-        vsum(("cnt", v, v + 1), ("cmp", 128 * (v - VS), 128 * (v - VS) + 128))
-    for e in range(2):
-        act(("x0", 16 * e + 1, 16 * e + 16, 2), ("cnt", 0, 8), AF.Copy, scale=U0)
-        vts(("x0", 16 * e, 16 * e + 16, 2), ("cnt", 0, 8), M0, None, OP.mult)
-    vtr(("xt0", 0, 32), ("x0", 0, 32))
-    for u in range(2):
-        vtt(("y0", u, 16, 2), ("xt0", 16 * u, 16 * u + 8), ("xt0", 16 * u + 8, 16 * u + 16), OP.add)
-    vts(("offs", 0, 16), ("y0", 0, 16), AL, BE, OP.mult, OP.add)
+    vset(("zr", 0, 512), 0.0)
+    act(("zb", 32, 544), ("zr", 0, 512), AF.Copy)
+    book("b1")
+    vset(("xt", 512, 520), 0.0)
+    vset(("le", 0, 1), 0.0)
+    vset(("zt", 0, 16), 0.0)
+    vset(("onb", 0, 520), 1.0)
+    op("p", lambda: g.affine_select(T.gp[:, 0:520], T.onb[:, 0:520], [[-1, 520]], OP.is_equal, 0.0, 3, 4),
+       [("onb", 0, 520)], [("gp", 0, 520)])
+    act(("gm", 0, 520), ("gp", 0, 520), AF.Copy, scale=-1.0)
+    vts(T0, TOK, -128.0, None, OP.add)
+    vts(CHI, T0, M16, M16, OP.add, OP.subtract)
+    vtt(CLO, T0, CHI, OP.subtract)
+    vts(("tri", 0, 512, 4), ("itr", 0, 128), TOK, 2.0, OP.is_gt, OP.mult)
+    vts(("tri", 1, 512, 4), ("itr", 0, 128), TOK, None, OP.is_equal)
+    vset(("zb", 514, 544, 4), -15.0)
+    vcopy(("zb", 513, 544, 4), ("c256", 0, 8))
+    quant("qc", 0, ("zb", 0, 512))
+    vts(("tri", 2, 512, 4), ("itr", 0, 128), TOK, None, OP.is_equal)
+    vset(("tri", 3, 512, 4), 0.0)
+
+    quant("qx", 0, ("xt", 0, 520))
+    mm("sc", 0, "qx", 0, "qc", 0)
+    quant("qtri", 0, ("tri", 0, 512))
+    vscan(("pmc", 0, 8), ("zt", 0, 8), ("sc", 0, 8), BIG, OP.add, OP.max)
+    vts(("le", 1, 9), ("pmc", 0, 8), ("pmc", 7, 8), None, OP.is_ge)
+    vtt(("zb", 512, 544, 4), ("le", 1, 9), ("le", 0, 8), OP.subtract)
+    quant("qo", 0, ("zb", 32, 544))
+    mm("sc", 1, "qtri", 0, "qo", 0)
+    for l in ("lv1", "lv2"):
+        dma("y", u8(T, l, 256, 258), u8(T, "qx", 128, 130), [("qx", 128, 130)], [(l, 256, 258)])
+        dma("y", T[l + "_s"][:, 256:258], T["qx_s"][:, 128:130], [("qx_s", 128, 130)], [(l + "_s", 256, 258)])
+    vset(("sx", 0, 576), 0.0)
+    vtt(("g8", 0, 8), ("zb", 512, 544, 4), ("sc", 632, 640), OP.mult)
+    vsum(G, ("g8", 0, 8))
+    vts(FH, G, M32, M32, OP.add, OP.subtract)
+    vts(("sx", 0, 512, 4), ("ir", 0, 128), FH, G, OP.add, OP.is_equal)
+    vts(("sx", 1, 512, 4), ("ir", 0, 128), FH, G, OP.add, OP.is_equal)
+    vts(("sx", 512, 576, 4), ("ict", 0, 16), FH, CHI, OP.is_equal, OP.mult)
+    vts(("sx", 513, 576, 4), ("ict", 0, 16), FH, CLO, OP.is_equal, OP.mult)
+    quant("qs", 0, ("sx", 0, 576))
+    mm("sc", 2, "qs", 0, "qs", 16)
+    vset(("rst", 0, 256), 0.0)
+    vts(("offs", 0, 16), ("sc", 1136, 1152), 128.0, None, OP.add)
 
     def to_relays(kind, buf, w, dstbuf, sem):
         codes = SCRATCH[buf][2] == F8
@@ -424,14 +435,10 @@ def home_program(g, core, T, topo):
                 parts.append((dc, es, sem, T[dstbuf][:, a:a + w], T[buf][:, w * k:w * k + w]))
         fused([(buf, 0, 4 * w)], parts)
 
-    for i in range(2):
-        k = pl["far"][i][0] // 2
-        pick("sf", 64 * i, "qx", 130, "offs", 4 * k, 4 * k + 4)
+    pick("sf", 0, "qx", 130, "offs", 0, 8)
     to_relays("codes", "sf", 64, "rz", "rzc")
     to_relays("scales", "sf_s", 64, "rz_s", "rzs")
-    for i in range(2):
-        k = pl["near"][i][0] // 2
-        pick("sn", 64 * i, "qx", 130, "offs", 4 * k, 4 * k + 4)
+    pick("sn", 0, "qx", 130, "offs", 8, 16)
 
     def at_near(d):
         p = plan(T, topo, T.cores[d])
@@ -443,88 +450,80 @@ def home_program(g, core, T, topo):
         dma("y", u8(T, dst, d0, d0 + 32), u8(T, src, s0, s0 + 32), [(src, s0, s0 + 32)], [(dst, d0, d0 + 32)])
         dma("y", T[dst + "_s"][:, d0:d0 + 32], T[src + "_s"][:, s0:s0 + 32], [(src + "_s", s0, s0 + 32)], [(dst + "_s", d0, d0 + 32)])
     keep("zn", 32 * own, "sn", 32 * own)
+    book("b2")
 
-    vts(("mk", 0, 32), ("hp", 0, 32), HQ, None, OP.is_equal)
-    vts(("a2", 0, 32), ("la0", 0, 32), R16, None, OP.add)
-    vtt(("a3", 0, 32), ("a2", 0, 32), ("mk", 0, 32), OP.mult)
-    vts(("offd", 0, 32), ("a3", 0, 32), 128.0, None, OP.add)
+    for k, (sh, m) in enumerate(((0, 15), (5, 7), (4, 1), (4, 7), (0, 3))):
+        o = ("ic", k, k + 1)
+        if sh:
+            vts(o, ("ip", 0, 1), sh, m, OP.arith_shift_right, OP.bitwise_and)
+        else:
+            vts(o, ("ip", 0, 1), m, None, OP.bitwise_and)
+    vcopy(("cf", 0, 5), ("ic", 0, 5))
+    vts(HQ128, HQ, 128.0, None, OP.mult)
     vts(E0, U1, -1.0, 1.0, OP.mult, OP.add)
-    quant("qb1", 0, ("b1t", 0, 512))
-    quant("zn", 128, ("zt", 0, 512))
-    quant("zf", 128, ("zt", 0, 512))
-    vts(("gm", 0, 520), ("gp", 0, 520), -1.0, None, OP.mult)
-    for b in range(4):
-        quant("qe", 128 * b, ("gp", 3 - b, 515 - b))
-        quant("qm", 128 * b, ("gm", 3 - b, 515 - b))
-    quant("rqn", 128, ("zt", 0, 512))
-    quant("rqf", 128, ("zt", 0, 512))
-    quant("qb2", 0, ("b2t", 0, 512))
-    for x in ("n", "f", "h"):
-        vset(("xs" + x, 0, 32), 0.0)
+    vset(("rst", 0, 256, 128), BIG)
+    for h in range(4):
+        vts(("w16", 128 * h, 128 * h + 128), ("ik", 0, 128), -64.0 * h, R16, OP.add, OP.is_equal)
+    quant("qw16", 0, ("w16", 0, 512))
+    vts(("mxx", 0, 64), ("imx", 0, 64), P16, None, OP.is_equal)
+    vts(("offc", 0, 4), ("ioc", 0, 4), P3, None, OP.add)
+    vset(("xb", 64, 544), 0.0)
 
-    def spread(x, i, out, plus):
-        s = "xs" + x
-        act((s, 0, 8, 2), i, AF.Copy, scale=E0)
-        act((s, 1, 8, 2), i, AF.Copy, scale=U1)
-        yield
-        vtr((s, 32, 64), (s, 0, 32))
-        yield
-        vtt((s, 64, 80), (s, 32, 48), (s, 48, 64), OP.add)
-        vtt((s, 80, 96), (s, 32, 48), (s, 48, 64), OP.add)
-        yield
-        vtr((s, 96, 128), (s, 64, 96))
-        yield
-        vts((out, 0, 8), (s, 96, 104), plus, None, OP.add)
+    def relocate(x, n4, bank):
+        hl, ql, v = "hl" + x, "ql" + x, (544 if x == "n" else 0)
+        vts((hl, 0, 4), (n4, 0, 4), M16, M16, OP.add, OP.subtract)
+        vtt((hl, 4, 8), (n4, 0, 4), (hl, 0, 4), OP.subtract)
+        o, w, f, m = ("xb", v, v + 64), (hl, 0, 8), ("offc", 0, 4), ("mxx", 0, 64)
+        op("v", lambda: g.vector.tensor_tensor(ap(o), ap(w).indirect(ap(f)), ap(m), OP.mult), [w, f, m], [o])
+        a = 64 if x == "n" else 0
+        quant(ql, 0, ("xb", a, a + 544))
+        mm("sc", bank, "qw16", 0, ql, 0, True, False)
+        mm("sc", bank, "qw16", 0, ql, 8, False, True)
+        k = 512 * bank + (120 if x == "n" else 0)
+        return ("sc", k, k + 8)
 
-    vtt(MU, M0, E0, OP.mult)
-    vts(DC, D8, 32.0, -257.0, OP.mult, OP.add)
-    vts(("t1", 0, 128), ("inc", 0, 128), 32.5, MU, OP.is_le, OP.mult)
-    vts(("t3", 0, 128), ("inc", 0, 128), DC, None, OP.add)
-    vtt(("t2", 0, 128), ("t1", 0, 128), ("ohf", 0, 128), OP.mult)
-    vtt(("t4", 0, 128), ("t2", 0, 128), ("t3", 0, 128), OP.mult)
-    vtr(("t1", 0, 128), ("t4", 0, 128))
-    for b in range(4):
-        vsum(("sl", b, b + 1), ("t1", 32 * b, 32 * b + 32))
-    for _ in spread("h", ("sl", 0, 4), "offh", 256.0):
-        pass
-    quant("lv1", 256, ("zt", 0, 512))
-    quant("lv2", 256, ("zt", 0, 512))
-    quant("qw", 0, ("wt", 0, 512))
-    vset(("xw", 0, 512), 0.0)
-    vset(("xtw", 256, 288), -1.0)
-    vset(("xtw", 544, 576), -1.0)
+    def home_list():
+        vts(T0, G, -112.0, M256, OP.add, OP.add)
+        vts(T1, T0, M256, 0.25, OP.subtract, OP.mult)
+        vts(T2, T1, -4.0, G, OP.mult, OP.add)
+        vts(T3, T2, 2.0 * CAPP - 16, 0.5, OP.is_lt, OP.mult)
+        vts(T4, T2, T1, 15.0 - 512.0, OP.add, OP.add)
+        vtt(T5, T4, T3, OP.mult)
+        vts(("n4h", 0, 4), ("zt", 0, 4), T5, None, OP.add)
+        ls = relocate("n", "n4h", 3)
+        vts(("offh", 0, 8), ls, 256.0, None, OP.add)
 
     def level(x, l):
-        win, book, dg, pm, nn, off = ("z" if l == 1 else "rq") + x, "qb%d" % l, "dg%d%s" % (l, x), "pm" + x, "nn" + x, "off%d%s" % (l, x)
-        turn = 2 if (x, l) == ("n", 2) else 0
+        win, bk, pm, n4, nn, off, sa = ("z" if l == 1 else "rq") + x, "qb%d" % l, "pm" + x, "n4" + x, "nn" + x, "off%d%s" % (l, x), "sa" + x
+        b0 = 0 if x == "n" else 2
+        ls = []
 
-        def codes(p):
-            pick_codes(dg, 256 * p, win, 130, "offd", 16 * p, 16 * p + 16)
+        def score():
+            for i in range(2):
+                mm("sc", b0 + i, win, 0, bk, 256 * i, True, True, 256)
 
-        def scales(p):
-            pick_scales(dg, 256 * p, win, 130, "offd", 16 * p, 16 * p + 16)
+        def scan(i):
+            k = 512 * (b0 + i)
+            vscan((pm, 256 * i, 256 * i + 256), ("rst", 0, 256), ("sc", k, k + 256), 0.0, OP.add, OP.max)
 
-        def score(p):
-            for b in range(2 * p, 2 * p + 2):
-                mm("sc", (b + turn) % 4, dg, 128 * b, book, 0)
+        def tally(i):
+            for h in range(2 * i, 2 * i + 2):
+                act(("jk", 128 * h, 128 * h + 128), (pm, 128 * h, 128 * h + 128), AF.Sign, bias=(pm, 128 * h + 127, 128 * h + 128),
+                    scale=-1.0, acc=(n4, h, h + 1))
 
-        def best(b):
-            p, k = (pm, 128 * b, 128 * b + 128), 512 * ((b + turn) % 4)
-            vscan(p, ("zt", 0, 128), ("sc", k, k + 128), BIG, OP.add, OP.max)
-            act(("jk", 128 * b, 128 * b + 128), p, AF.Sign, bias=(pm, 128 * b + 127, 128 * b + 128), scale=-1.0,
-                acc=(nn, 2 * b + l - 1, 2 * b + l))
-
-        def words():
-            for _ in spread(x, (nn, l - 1, 8, 2), off, 0.0):
-                yield
+        def place():
+            ls.append(relocate(x, n4, b0))
 
         def take():
-            pick("v%d%s" % (l, x), 0, book, 128, off, 0, 8)
-        return codes, scales, score, best, words, take
+            vts((off, 0, 8), ls[0], HQ128, None, OP.add)
+            pick("v%d%s" % (l, x), 0, bk, 512, off, 0, 8)
 
-    def run(gen):
-        for _ in gen:
-            pass
+        def number():
+            a, b = ls[0][1], ls[0][2]
+            act((sa, 0, 4), ("sc", a, b, 2), AF.Copy, scale=E0)
+            act((sa, 4, 8), ("sc", a + 1, b, 2), AF.Copy, scale=U1)
+            vtt((nn, l - 1, 8, 2), (sa, 0, 4), (sa, 4, 8), OP.add)
+        return score, scan, tally, place, take, number
 
     def back(x, l):
         v, lv = "v%d%s" % (l, x), "lv%d" % l
@@ -536,56 +535,53 @@ def home_program(g, core, T, topo):
             to_near(v + "_s", 32, lv + "_s", lambda d: 32 * me, "hv%dn" % l, near)
             keep(lv, 32 * me, v, 32 * own)
 
-    n2codes, n2scales, n2score, n2best, n2words, n2take = level("n", 2)
-    for x in ("n", "f"):
-        codes, scales, score, best, words, take = level(x, 1)
-        for p in range(2):
-            codes(p)
-            scales(p)
-            score(p)
-        for b in range(4):
-            best(b)
+    def given(x):
         for b in range(4):
             mm("dd", b, "qe", 128 * b, "z" + x, 0, True, False)
-        run(words())
-        take()
-        back(x, 1)
-        rt = "rt" + x
+
+    def minus(x):
         for b in range(4):
             mm("dd", b, "qm", 128 * b, "v1" + x, 0, False, True)
-        if x == "f":
-            n2codes(0)
+
+    def rest(x):
+        rt = "rt" + x
         vcopy((rt, 0, 512, 4), ("dd", 0, 128))
         act((rt, 1, 512, 4), ("dd", 512, 640), AF.Copy)
         vcopy((rt, 2, 512, 4), ("dd", 1024, 1152))
         act((rt, 3, 512, 4), ("dd", 1536, 1664), AF.Copy)
-        if x == "f":
-            n2scales(0)
-        quant("rq" + x, 0, (rt, 0, 512))
-    codes, scales, score, best, words, take = level("f", 2)
-    for p in range(2):
-        codes(p)
-        scales(p)
-        score(p)
-    for b in range(4):
-        best(b)
-    n2score(0)
-    for k, _ in enumerate(words()):
-        if k == 0:
-            n2codes(1)
-            n2scales(1)
-            n2score(1)
-    take()
-    to_relays("scales", "nnf", 4, "rn", "rnc")
-    back("f", 2)
-    for b in range(4):
-        n2best(b)
-    run(n2words())
-    n2take()
-    dma("y", T.lan[:, 2 * me:2 * me + 2], T.nnn[:, 2 * own:2 * own + 2], [("nnn", 2 * own, 2 * own + 2)], [("lan", 2 * me, 2 * me + 2)])
-    to_relays("codes", "nnn", 2, "rp", "rpn")
-    back("n", 2)
-    to_near("nnn", 2, "lan", lambda d: 2 * me, "hnn", pl["near"][1])
+
+    def constants(q, t):
+        for b in range(4):
+            quant(q, 128 * b, (t, 3 - b, 515 - b))
+
+    def own_numbers():
+        to_near("nnn", 2, "lan", lambda d: 2 * me, "hnn", pl["near"][1])
+        dma("y", T.lan[:, 2 * me:2 * me + 2], T.nnn[:, 2 * own:2 * own + 2], [("nnn", 2 * own, 2 * own + 2)], [("lan", 2 * me, 2 * me + 2)])
+
+    def last():
+        vset(("xw", 0, 256), 0.0)
+        vset(("xtw", 256, 288), -1.0)
+
+    def steps():
+        d = {}
+        for x in "nf":
+            for l in (1, 2):
+                score, scan, tally, place, take, number = level(x, l)
+                k = x.upper() + str(l) + "."
+                d.update({k + "score": score, k + "scan0": lambda f=scan: f(0), k + "scan1": lambda f=scan: f(1),
+                          k + "count0": lambda f=tally: f(0), k + "count1": lambda f=tally: f(1), k + "place": place,
+                          k + "take": take, k + "number": number, k + "back": lambda x=x, l=l: back(x, l)})
+            d.update({x + ".given": lambda x=x: given(x), x + ".minus": lambda x=x: minus(x), x + ".rest": lambda x=x: rest(x),
+                      x + ".repack": lambda x=x: quant("rq" + x, 0, ("rt" + x, 0, 512))})
+        d.update({"qe": lambda: constants("qe", "gp"), "qm": lambda: constants("qm", "gm"), "hl": home_list, "fin": last,
+                  "qb1": lambda: quant("qb1", 0, ("b1t", 0, 2048)), "qb2": lambda: quant("qb2", 0, ("b2t", 0, 2048)),
+                  "qw": lambda: quant("qw", 0, ("wt", 0, 512)), "f.nums": lambda: to_relays("scales", "nnf", 4, "rn", "rnc"),
+                  "n.nums1": lambda: to_relays("codes", "nnn", 2, "rp", "rpn"), "n.nums2": own_numbers})
+        return d
+
+    todo = steps()
+    for name in ORDER.split():
+        todo[name]()
 
     def store(l):
         h = "h%d" % l
@@ -596,22 +592,19 @@ def home_program(g, core, T, topo):
 
     pick("h1", 0, "lv1", 258, "offh", 0, 8)
     store(1)
-    mm("sc", 0, "qw", 0, "h1", 0, True, False)
+    mm("sc", 3, "qw", 0, "h1", 0, True, False)
     pick("h2", 0, "lv2", 258, "offh", 0, 8)
-    mm("sc", 0, "qw", 0, "h2", 0, False, True)
+    mm("sc", 3, "qw", 0, "h2", 0, False, True)
     store(2)
     for l in range(2):
-        vcopy(("xw", 256 * l, 256 * l + 256, 32), ("lan", l, 16, 2))
-    for l in range(2):
-        vtr(("xtw", 288 * l, 288 * l + 256), ("xw", 256 * l, 256 * l + 256))
-    act(("yt", 0, 128), ("sc", 0, 128), AF.Copy)
+        vcopy(("xw", l, 256, 32), ("lan", l, 16, 2))
+    vtr(("xtw", 0, 256), ("xw", 0, 256))
+    act(("yt", 0, 128), ("sc", 1536, 1664), AF.Copy)
     dma("s", T.y[:], T.yt[:], [("yt", 0, 128)], [], True)
     o, w, f = ("wnt", 0, 128), ("xtw", 0, 288), ("offh", 0, 8)
     op("v", lambda: g.vector.tensor_copy(ap(o), ap(w).indirect(ap(f))), [w, f], [o])
-    dma("y", T.wn[0:4, :], T.wnt[0:128:32, 0:128], [o], [], True)
-    o2, w2 = ("wnt", 128, 256), ("xtw", 288, 576)
-    op("s", lambda: g.scalar.activation(ap(o2), ap(w2).indirect(ap(f)), AF.Copy), [w2, f], [o2])
-    dma("s", T.wn[4:8, :], T.wnt[0:128:32, 128:256], [o2], [], True)
+    for l in range(2):
+        dma("ys"[l], T.wn[4 * l:4 * l + 4, :], T.wnt[l:128:32, 0:128], [o], [], True)
     for s in total:
         if waited.get(s, 0) < total[s]:
             g.wait_ge(T.sem[s], total[s])

@@ -24,38 +24,41 @@ for _n, _w in (("qx", 130), ("qc", 128), ("qo", 128), ("qtri", 128), ("qs", 144)
                ("lv1", 384), ("lv2", 384), ("h1", 128), ("h2", 128), ("rz", 64), ("rv1", 64), ("rv2", 64)):
     _codes(_n, _w)
 for _n, _w in (("xt", 520), ("zr", 512), ("zb", 544), ("xb", 608), ("sx", 576), ("b1t", 2048), ("b2t", 2048), ("wt", 512), ("onb", 520),
-               ("gp", 520), ("gm", 520), ("tri", 512), ("w16", 512), ("ir", 128), ("itr", 128), ("ik", 128), ("imx", 64), ("mxx", 64),
+               ("gp", 520), ("gm", 520), ("tri", 512), ("w16", 512), ("ir", 128), ("itr", 128), ("ik", 128), ("imx", 32), ("mxx", 32),
                ("ict", 16), ("rst", 256), ("jk", 512), ("rtn", 512), ("rtf", 512), ("xw", 256), ("xtw", 288)):
     _buf(_n, _w, "bfloat16")
-for _n, _w in (("pmn", 512), ("pmf", 512), ("cf", 32), ("c256", 8), ("ioc", 4), ("tok", 1), ("pmc", 8), ("le", 16), ("g8", 8),
-               ("n4n", 4), ("n4f", 4), ("n4h", 4), ("hln", 8), ("hlf", 8), ("zt", 16), ("san", 8), ("saf", 8),
-               ("nnn", 8), ("nnf", 8), ("rn", 4), ("rp", 2), ("lan", 16), ("wnt", 128), ("yt", 128)):
+for _n, _w in (("pmn", 512), ("pmf", 512), ("cf", 32), ("c256", 8), ("tok", 1), ("pmc", 8), ("le", 16), ("g8", 8),
+               ("n4n", 4), ("n4f", 4), ("n4h", 4), ("xmn", 32), ("xmf", 32), ("zt", 16), ("san", 8), ("saf", 8),
+               ("nnn", 8), ("nnf", 8), ("rn", 4), ("lan", 16), ("wnt", 128), ("yt", 128)):
     _buf(_n, _w)
 _buf("ip", 1, "int32")
 _buf("ic", 8, "int32")
-for _n, _w in (("offc", 4), ("offs", 16), ("offh", 8), ("off1n", 8), ("off1f", 8), ("off2n", 8), ("off2f", 8)):
+for _n, _w in (("offc", 2), ("offs", 16), ("offh", 8), ("off1n", 8), ("off1f", 8), ("off2n", 8), ("off2f", 8)):
     _buf(_n, _w, "uint16")
 SCRATCH["sc"] = ("psum", [128, 2048], "float32")
 SCRATCH["dd"] = ("psum", [128, 2048], "float32")
 
 SEMAPHORES = (["ev", "es", "et", "ep", "sent", "st"] + ["l%d" % i for i in range(40)]
               + ["azn", "azf", "hv1n", "hv1f", "hv2n", "hv2f", "hnn", "hnf"]
-              + ["rzc", "rzs", "r1c", "r1s", "rnc", "r2c", "r2s", "rpn"])
+              + ["rzc", "rzs", "r1c", "r1s", "rnc", "r2c", "r2s"])
 
 CAPP = 32
 FN = 4
 FM = 8
 FF = 4
 FR = 4
-FP = 8
 BIG = -9e29
 M16, M32, M256 = 1.5 * 2.0 ** 27, 1.5 * 2.0 ** 28, 1.5 * 2.0 ** 31
 PLANS = {}
+HS0, HS1 = (0,), (1, 2, 3)
 ORDER = """
-hl qb1 qe N1.score N1.scan0 N1.count0 N1.scan1 N1.count1 n.given N1.place qm F1.score N1.take n.minus F1.scan0 qb2 F1.count0
-n.rest F1.scan1 N1.number f.given F1.count1 n.repack N2.score F1.place N2.scan0 N2.count0 N2.scan1 F1.take N2.count1 f.minus
-N2.place f.rest N1.back f.repack F1.number N2.take F2.score F2.scan0 F1.back F2.count0 F2.scan1 F2.count1 F2.place N2.number
-N2.back F2.take F2.back qw F2.number f.nums n.nums1 n.nums2 fin"""
+qm2 qe0 qb1 qe1 qe3 qm3 N1.score qm0 N1.scan0 N1.scan1 N1.count0 qm1 N1.count1 F1.score qe2 N1.place0 N1.place1 N1.place2
+N1.place3 N1.place4 qb2 n.given N1.list N1.codes N1.scales n.minus F1.scan0 N1.parts F1.scan1 F1.count0 n.rest0 n.rest1 n.rest2
+n.rest3 n.repack F1.count1 F1.place0 F1.place1 N2.score F1.place2 N2.scan0 F1.place3 N2.count0 F1.place4 f.given N2.scan1
+N2.count1 F1.list F1.codes F1.scales f.minus N2.place0 N1.codesback N2.place1 N1.scalesback F1.parts N2.place2 f.rest0
+F1.codesback f.rest1 N2.place3 f.rest2 F1.number N1.number f.rest3 f.repack F1.scalesback N2.place4 F2.score N2.list N2.codes
+N2.parts N2.scales F2.scan0 F2.scan1 F2.count0 N2.number F2.count1 F2.place0 N2.scalesback F2.place1 N2.codesback F2.place2
+F2.place3 qw F2.place4 F2.list F2.scales F2.parts F2.codes n.nums F2.number F2.codesback F2.scalesback fin hl f.nums"""
 
 
 def plan(T, topo, core):
@@ -105,13 +108,13 @@ def u8(T, name, a, b):
 
 
 def relay_program(g, core, T, topo):
-    src, grp, role, to = None, None, None, None
+    src, grp, role = None, None, None
     for c in T.cores:
         p = plan(T, topo, c)
         for i in range(2):
             for k in ("codes", "scales"):
                 if p[k][i] == core:
-                    src, grp, role, to = T.rank_of(c), p["far"][i], k, p["near"][0][i]
+                    src, grp, role = T.rank_of(c), p["far"][i], k
     if src is None:
         return
     sent = [0]
@@ -134,16 +137,11 @@ def relay_program(g, core, T, topo):
         hand("rzc", "azf", lambda j, at: (u8(T, "zf", 32 * at, 32 * at + 32), u8(T, "rz", 32 * j, 32 * j + 32)))
         hand("r1c", "hv1f", lambda j, at: (u8(T, "lv1", o, o + 32), u8(T, "rv1", 32 * j, 32 * j + 32)))
         hand("r2c", "hv2f", lambda j, at: (u8(T, "lv2", o, o + 32), u8(T, "rv2", 32 * j, 32 * j + 32)))
-        g.wait_ge(T.sem.rpn, FF)
-        dst = T.cores[to]
-        es = topo.engines(core, dst)[:FP]
-        g.remote_dma_fused([xfer(T, topo, core, dst, es, "hnn", T["lan"][:, 2 * src:2 * src + 2], T["rp"][:, 0:2])], local_sem=T.sem.sent)
-        sent[0] += FP
+        hand("rnc", "hnf", lambda j, at: (T["lan"][:, 2 * src:2 * src + 2], T["rn"][:, 2 * j:2 * j + 2]))
     else:
         hand("rzs", "azf", lambda j, at: (T["zf_s"][:, 32 * at:32 * at + 32], T["rz_s"][:, 32 * j:32 * j + 32]))
         hand("r1s", "hv1f", lambda j, at: (T["lv1_s"][:, o:o + 32], T["rv1_s"][:, 32 * j:32 * j + 32]))
         hand("r2s", "hv2f", lambda j, at: (T["lv2_s"][:, o:o + 32], T["rv2_s"][:, 32 * j:32 * j + 32]))
-        hand("rnc", "hnf", lambda j, at: (T["lan"][:, 2 * src:2 * src + 2], T["rn"][:, 2 * j:2 * j + 2]))
     g.wait_ge(T.sem.sent, sent[0])
 
 
@@ -306,10 +304,10 @@ def home_program(g, core, T, topo):
     dma("s", T.zb[:, 0:32], T.co[:, 0:32], [], [("zb", 0, 32)])
     dma("y", T.wt[:], T.w[:], [], [("wt", 0, 512)])
 
-    def book(b):
-        for h in range(4):
+    def book(b, hs=range(4)):
+        for h in hs:
             act((b + "t", 512 * h, 512 * h + 512), ("zr", 0, 512), AF.Copy)
-        for h in range(4):
+        for h in hs:
             dma("y", T[b + "t"][32 * h:32 * h + 32, 512 * h:512 * h + 512], T[b][32 * h:32 * h + 32, :], [], [(b + "t", 512 * h, 512 * h + 512)])
 
     near, far = pl["near"][0] + pl["near"][1], pl["far"][0] + pl["far"][1]
@@ -329,7 +327,7 @@ def home_program(g, core, T, topo):
     arrive("azn", 2 * from_near, nw)
     arrive("hv1n", 2 * from_near, hw1)
     arrive("hv2n", 2 * from_near, hw2)
-    arrive("hnn", 2 * FP + FM, nn_)
+    arrive("hnn", from_near, nn_)
     arrive("azf", 4 * 2 * FR, both("zf", 0, 128))
     hw1, hw2, nn_ = [], [], []
     for r in far:
@@ -360,19 +358,18 @@ def home_program(g, core, T, topo):
     iota(("ict", 8, 16), [[512 * (pn[1] - pn[0]), 2], [256, 2], [32, 2]], 512 * pn[0], 0)
     iota(("ip", 0, 1), [[1, 1]], 0, 1)
     iota(("ik", 0, 128), [[0, 2], [1, 16], [64, 4]], 0, 0)
-    iota(("imx", 0, 64), [[0, 2], [1, 8], [0, 4]], 0, 0)
-    iota(("ioc", 0, 4), [[4, 2], [0, 2]], 0, 0)
+    iota(("imx", 0, 32), [[1, 8], [0, 4]], 0, 0)
 
     vset(("zr", 0, 512), 0.0)
     act(("zb", 32, 544), ("zr", 0, 512), AF.Copy)
     book("b1")
+    book("b2", HS0)
     vset(("xt", 512, 520), 0.0)
     vset(("le", 0, 1), 0.0)
     vset(("zt", 0, 16), 0.0)
     vset(("onb", 0, 520), 1.0)
     op("p", lambda: g.affine_select(T.gp[:, 0:520], T.onb[:, 0:520], [[-1, 520]], OP.is_equal, 0.0, 3, 4),
        [("onb", 0, 520)], [("gp", 0, 520)])
-    act(("gm", 0, 520), ("gp", 0, 520), AF.Copy, scale=-1.0)
     vts(T0, TOK, -128.0, None, OP.add)
     vts(CHI, T0, M16, M16, OP.add, OP.subtract)
     vtt(CLO, T0, CHI, OP.subtract)
@@ -395,7 +392,8 @@ def home_program(g, core, T, topo):
     for l in ("lv1", "lv2"):
         dma("y", u8(T, l, 256, 258), u8(T, "qx", 128, 130), [("qx", 128, 130)], [(l, 256, 258)])
         dma("y", T[l + "_s"][:, 256:258], T["qx_s"][:, 128:130], [("qx_s", 128, 130)], [(l + "_s", 256, 258)])
-    vset(("sx", 0, 576), 0.0)
+    vset(("sx", 2, 576, 4), 0.0)
+    vset(("sx", 3, 576, 4), 0.0)
     vtt(("g8", 0, 8), ("zb", 512, 544, 4), ("sc", 632, 640), OP.mult)
     vsum(G, ("g8", 0, 8))
     vts(FH, G, M32, M32, OP.add, OP.subtract)
@@ -420,11 +418,11 @@ def home_program(g, core, T, topo):
                 parts.append((rc, es[k:k + FF], sem, T[dstbuf][:, 0:w], T[buf][:, w * i:w * i + w]))
         fused([(buf, 0, 2 * w)], parts)
 
-    def to_near(buf, w, dstbuf, place, sem, some):
+    def to_near(buf, w, dstbuf, place, sem):
         codes = SCRATCH[buf][2] == F8
         parts = []
         for k, d in enumerate(near):
-            if d == me or d not in some:
+            if d == me:
                 continue
             a, dc, n = place(d), T.cores[d], len(parts)
             es = topo.engines(core, dc)
@@ -443,14 +441,15 @@ def home_program(g, core, T, topo):
     def at_near(d):
         p = plan(T, topo, T.cores[d])
         return 32 * (p["near"][0] + p["near"][1]).index(me)
-    to_near("sn", 32, "zn", at_near, "azn", near)
-    to_near("sn_s", 32, "zn_s", at_near, "azn", near)
+    to_near("sn", 32, "zn", at_near, "azn")
+    to_near("sn_s", 32, "zn_s", at_near, "azn")
 
     def keep(dst, d0, src, s0):
         dma("y", u8(T, dst, d0, d0 + 32), u8(T, src, s0, s0 + 32), [(src, s0, s0 + 32)], [(dst, d0, d0 + 32)])
         dma("y", T[dst + "_s"][:, d0:d0 + 32], T[src + "_s"][:, s0:s0 + 32], [(src + "_s", s0, s0 + 32)], [(dst + "_s", d0, d0 + 32)])
     keep("zn", 32 * own, "sn", 32 * own)
-    book("b2")
+    book("b2", HS1)
+    act(("gm", 0, 520), ("gp", 0, 520), AF.Copy, scale=-1.0)
 
     for k, (sh, m) in enumerate(((0, 15), (5, 7), (4, 1), (4, 7), (0, 3))):
         o = ("ic", k, k + 1)
@@ -465,22 +464,25 @@ def home_program(g, core, T, topo):
     for h in range(4):
         vts(("w16", 128 * h, 128 * h + 128), ("ik", 0, 128), -64.0 * h, R16, OP.add, OP.is_equal)
     quant("qw16", 0, ("w16", 0, 512))
-    vts(("mxx", 0, 64), ("imx", 0, 64), P16, None, OP.is_equal)
-    vts(("offc", 0, 4), ("ioc", 0, 4), P3, None, OP.add)
+    vts(("mxx", 0, 32), ("imx", 0, 32), P16, None, OP.is_equal)
+    vts(("offc", 0, 2), ("zt", 0, 2), P3, None, OP.add)
     vset(("xb", 64, 544), 0.0)
 
     def relocate(x, n4, bank):
-        hl, ql, v = "hl" + x, "ql" + x, (544 if x == "n" else 0)
-        vts((hl, 0, 4), (n4, 0, 4), M16, M16, OP.add, OP.subtract)
-        vtt((hl, 4, 8), (n4, 0, 4), (hl, 0, 4), OP.subtract)
-        o, w, f, m = ("xb", v, v + 64), (hl, 0, 8), ("offc", 0, 4), ("mxx", 0, 64)
-        op("v", lambda: g.vector.tensor_tensor(ap(o), ap(w).indirect(ap(f)), ap(m), OP.mult), [w, f, m], [o])
+        ql, v = "ql" + x, (544 if x == "n" else 0)
+        o, w, f, m = ("xm" + x, 0, 32), (n4, 0, 4), ("offc", 0, 2), ("mxx", 0, 32)
         a = 64 if x == "n" else 0
-        quant(ql, 0, ("xb", a, a + 544))
-        mm("sc", bank, "qw16", 0, ql, 0, True, False)
-        mm("sc", bank, "qw16", 0, ql, 8, False, True)
         k = 512 * bank + (120 if x == "n" else 0)
-        return ("sc", k, k + 8)
+
+        def spread():
+            op("v", lambda: g.vector.tensor_tensor(ap(o), ap(w).indirect(ap(f)), ap(m), OP.mult), [w, f, m], [o])
+
+        def products():
+            mm("sc", bank, "qw16", 0, ql, 0, True, False)
+            mm("sc", bank, "qw16", 0, ql, 8, False, True)
+        return (spread, lambda: vts(("xb", v, v + 32), o, M16, M16, OP.add, OP.subtract),
+                lambda: vtt(("xb", v + 32, v + 64), o, ("xb", v, v + 32), OP.subtract),
+                lambda: quant(ql, 0, ("xb", a, a + 544)), products), ("sc", k, k + 8)
 
     def home_list():
         vts(T0, G, -112.0, M256, OP.add, OP.add)
@@ -490,13 +492,17 @@ def home_program(g, core, T, topo):
         vts(T4, T2, T1, 15.0 - 512.0, OP.add, OP.add)
         vtt(T5, T4, T3, OP.mult)
         vts(("n4h", 0, 4), ("zt", 0, 4), T5, None, OP.add)
-        ls = relocate("n", "n4h", 3)
+        fs, ls = relocate("n", "n4h", 3)
+        for f in fs:
+            f()
         vts(("offh", 0, 8), ls, 256.0, None, OP.add)
 
     def level(x, l):
         win, bk, pm, n4, nn, off, sa = ("z" if l == 1 else "rq") + x, "qb%d" % l, "pm" + x, "n4" + x, "nn" + x, "off%d%s" % (l, x), "sa" + x
         b0 = 0 if x == "n" else 2
-        ls = []
+        fs, ls = relocate(x, n4, b0)
+        a, b = ls[1], ls[2]
+        v = ("v%d%s" % (l, x), 0, bk, 512, off, 0, 8)
 
         def score():
             for i in range(2):
@@ -511,28 +517,29 @@ def home_program(g, core, T, topo):
                 act(("jk", 128 * h, 128 * h + 128), (pm, 128 * h, 128 * h + 128), AF.Sign, bias=(pm, 128 * h + 127, 128 * h + 128),
                     scale=-1.0, acc=(n4, h, h + 1))
 
-        def place():
-            ls.append(relocate(x, n4, b0))
-
-        def take():
-            vts((off, 0, 8), ls[0], HQ128, None, OP.add)
-            pick("v%d%s" % (l, x), 0, bk, 512, off, 0, 8)
-
-        def number():
-            a, b = ls[0][1], ls[0][2]
+        def parts():
             act((sa, 0, 4), ("sc", a, b, 2), AF.Copy, scale=E0)
             act((sa, 4, 8), ("sc", a + 1, b, 2), AF.Copy, scale=U1)
-            vtt((nn, l - 1, 8, 2), (sa, 0, 4), (sa, 4, 8), OP.add)
-        return score, scan, tally, place, take, number
 
-    def back(x, l):
+        d = {"place%d" % i: f for i, f in enumerate(fs)}
+        for i in range(2):
+            d.update({"scan%d" % i: lambda i=i: scan(i), "count%d" % i: lambda i=i: tally(i)})
+        d.update({"score": score, "list": lambda: vts((off, 0, 8), ls, HQ128, None, OP.add), "codes": lambda: pick_codes(*v),
+                  "scales": lambda: pick_scales(*v), "parts": parts,
+                  "number": lambda: vtt((nn, l - 1, 8, 2), (sa, 0, 4), (sa, 4, 8), OP.add),
+                  "codesback": lambda: back(x, l, True), "scalesback": lambda: back(x, l, False)})
+        return d
+
+    def back(x, l, codes):
         v, lv = "v%d%s" % (l, x), "lv%d" % l
-        if x == "f":
+        if x == "f" and codes:
             to_relays("codes", v, 64, "rv%d" % l, "r%dc" % l)
+        elif x == "f":
             to_relays("scales", v + "_s", 64, "rv%d_s" % l, "r%ds" % l)
+        elif codes:
+            to_near(v, 32, lv, lambda d: 32 * me, "hv%dn" % l)
         else:
-            to_near(v, 32, lv, lambda d: 32 * me, "hv%dn" % l, near)
-            to_near(v + "_s", 32, lv + "_s", lambda d: 32 * me, "hv%dn" % l, near)
+            to_near(v + "_s", 32, lv + "_s", lambda d: 32 * me, "hv%dn" % l)
             keep(lv, 32 * me, v, 32 * own)
 
     def given(x):
@@ -543,19 +550,15 @@ def home_program(g, core, T, topo):
         for b in range(4):
             mm("dd", b, "qm", 128 * b, "v1" + x, 0, False, True)
 
-    def rest(x):
-        rt = "rt" + x
-        vcopy((rt, 0, 512, 4), ("dd", 0, 128))
-        act((rt, 1, 512, 4), ("dd", 512, 640), AF.Copy)
-        vcopy((rt, 2, 512, 4), ("dd", 1024, 1152))
-        act((rt, 3, 512, 4), ("dd", 1536, 1664), AF.Copy)
+    def rest(x, b):
+        o, i = ("rt" + x, b, 512, 4), ("dd", 512 * b, 512 * b + 128)
+        if b % 2:
+            act(o, i, AF.Copy)
+        else:
+            vcopy(o, i)
 
-    def constants(q, t):
-        for b in range(4):
-            quant(q, 128 * b, (t, 3 - b, 515 - b))
-
-    def own_numbers():
-        to_near("nnn", 2, "lan", lambda d: 2 * me, "hnn", pl["near"][1])
+    def near_numbers():
+        to_near("nnn", 2, "lan", lambda d: 2 * me, "hnn")
         dma("y", T.lan[:, 2 * me:2 * me + 2], T.nnn[:, 2 * own:2 * own + 2], [("nnn", 2 * own, 2 * own + 2)], [("lan", 2 * me, 2 * me + 2)])
 
     def last():
@@ -566,17 +569,18 @@ def home_program(g, core, T, topo):
         d = {}
         for x in "nf":
             for l in (1, 2):
-                score, scan, tally, place, take, number = level(x, l)
-                k = x.upper() + str(l) + "."
-                d.update({k + "score": score, k + "scan0": lambda f=scan: f(0), k + "scan1": lambda f=scan: f(1),
-                          k + "count0": lambda f=tally: f(0), k + "count1": lambda f=tally: f(1), k + "place": place,
-                          k + "take": take, k + "number": number, k + "back": lambda x=x, l=l: back(x, l)})
-            d.update({x + ".given": lambda x=x: given(x), x + ".minus": lambda x=x: minus(x), x + ".rest": lambda x=x: rest(x),
+                d.update({"%s%d.%s" % (x.upper(), l, n): f for n, f in level(x, l).items()})
+            d.update({x + ".given": lambda x=x: given(x), x + ".minus": lambda x=x: minus(x),
                       x + ".repack": lambda x=x: quant("rq" + x, 0, ("rt" + x, 0, 512))})
-        d.update({"qe": lambda: constants("qe", "gp"), "qm": lambda: constants("qm", "gm"), "hl": home_list, "fin": last,
+            for b in range(4):
+                d[x + ".rest%d" % b] = lambda x=x, b=b: rest(x, b)
+        for b in range(4):
+            d["qe%d" % b] = lambda b=b: quant("qe", 128 * b, ("gp", 3 - b, 515 - b))
+            d["qm%d" % b] = lambda b=b: quant("qm", 128 * b, ("gm", 3 - b, 515 - b))
+        d.update({"hl": home_list, "fin": last,
                   "qb1": lambda: quant("qb1", 0, ("b1t", 0, 2048)), "qb2": lambda: quant("qb2", 0, ("b2t", 0, 2048)),
-                  "qw": lambda: quant("qw", 0, ("wt", 0, 512)), "f.nums": lambda: to_relays("scales", "nnf", 4, "rn", "rnc"),
-                  "n.nums1": lambda: to_relays("codes", "nnn", 2, "rp", "rpn"), "n.nums2": own_numbers})
+                  "qw": lambda: quant("qw", 0, ("wt", 0, 512)), "f.nums": lambda: to_relays("codes", "nnf", 4, "rn", "rnc"),
+                  "n.nums": near_numbers})
         return d
 
     todo = steps()

from concourse.bass import DstId, RemoteDMATransfer
from concourse.mybir import dt, AluOpType, AxisListType, ActivationFunctionType

OP = AluOpType
AF = ActivationFunctionType
F8 = "float8_e4m3fn_x4"

SCRATCH = {}


def _codes(name, n):
    SCRATCH[name] = ("sbuf", [128, n], F8)
    SCRATCH[name + "_s"] = ("sbuf", [128, n], "uint8")


def _buf(name, n, ty="float32"):
    SCRATCH[name] = ("sbuf", [128, n], ty)


for _n, _w in (("qx", 130), ("qc", 128), ("qo", 128), ("qtri", 128), ("qs", 144), ("qw16", 128), ("qln", 136), ("qlf", 136),
               ("qb1", 512), ("qb2", 512), ("qw", 128), ("qe", 512), ("qm", 512),
               ("sf", 128), ("sn", 128), ("zn", 128), ("zf", 128),
               ("v1n", 128), ("v1f", 128), ("v2n", 128), ("v2f", 128), ("rqn", 128), ("rqf", 128),
               ("lv1", 384), ("lv2", 384), ("h1", 128), ("h2", 128), ("rz", 64), ("rv1", 64), ("rv2", 64)):
    _codes(_n, _w)
for _n, _w in (("xt", 520), ("zr", 512), ("zb", 544), ("xb", 608), ("sx", 576), ("b1t", 2048), ("b2t", 2048), ("wt", 512), ("onb", 520),
               ("gp", 520), ("gm", 520), ("tri", 512), ("w16", 512), ("ir", 128), ("itr", 128), ("ik", 128), ("imx", 32), ("mxx", 32),
               ("ict", 16), ("rst", 256), ("jk", 512), ("rtn", 512), ("rtf", 512), ("xw", 256), ("xtw", 288)):
    _buf(_n, _w, "bfloat16")
for _n, _w in (("pmn", 512), ("pmf", 512), ("cf", 32), ("c256", 8), ("tok", 1), ("pmc", 8), ("le", 16), ("g8", 8),
               ("n4n", 4), ("n4f", 4), ("n4h", 4), ("xmn", 32), ("xmf", 32), ("zt", 16), ("san", 8), ("saf", 8),
               ("nnn", 8), ("nnf", 8), ("rn", 4), ("lan", 16), ("wnt", 128), ("yt", 128)):
    _buf(_n, _w)
_buf("ip", 1, "int32")
_buf("ic", 8, "int32")
for _n, _w in (("offc", 2), ("offs", 16), ("offh", 8), ("off1n", 8), ("off1f", 8), ("off2n", 8), ("off2f", 8)):
    _buf(_n, _w, "uint16")
SCRATCH["sc"] = ("psum", [128, 2048], "float32")
SCRATCH["dd"] = ("psum", [128, 2048], "float32")

SEMAPHORES = (["ev", "es", "et", "ep", "sent", "st"] + ["l%d" % i for i in range(40)]
              + ["azn", "azf", "hv1n", "hv1f", "hv2n", "hv2f", "hnn", "hnf"]
              + ["rzc", "rzs", "r1c", "r1s", "rnc", "r2c", "r2s"])

CAPP = 32
FN = 4
FM = 8
FF = 4
FR = 4
BIG = -9e29
M16, M32, M256 = 1.5 * 2.0 ** 27, 1.5 * 2.0 ** 28, 1.5 * 2.0 ** 31
PLANS = {}
HS0, HS1 = (0,), (1, 2, 3)
ORDER = """
qm2 qe0 qb1 qe1 qe3 qm3 N1.score qm0 N1.scan0 N1.scan1 N1.count0 qm1 N1.count1 F1.score qe2 N1.place0 N1.place1 N1.place2
N1.place3 N1.place4 qb2 n.given N1.list N1.codes N1.scales n.minus F1.scan0 N1.parts F1.scan1 F1.count0 n.rest0 n.rest1 n.rest2
n.rest3 n.repack F1.count1 F1.place0 F1.place1 N2.score F1.place2 N2.scan0 F1.place3 N2.count0 F1.place4 f.given N2.scan1
N2.count1 F1.list F1.codes F1.scales f.minus N2.place0 N1.codesback N2.place1 N1.scalesback F1.parts N2.place2 f.rest0
F1.codesback f.rest1 N2.place3 f.rest2 F1.number N1.number f.rest3 f.repack F1.scalesback N2.place4 F2.score N2.list N2.codes
N2.parts N2.scales F2.scan0 F2.scan1 F2.count0 N2.number F2.count1 F2.place0 N2.scalesback F2.place1 N2.codesback F2.place2
F2.place3 qw F2.place4 F2.list F2.scales F2.parts F2.codes n.nums F2.number F2.codesback F2.scalesback fin hl f.nums"""


def plan(T, topo, core):
    if core in PLANS:
        return PLANS[core]
    cs = list(T.cores)
    here = [c for c in cs if c in topo.cores_of(core)]
    plane = [c for c in cs if c not in here and topo.same_plane(core, c)]
    far = [c for c in cs if c not in here and c not in plane]
    g0 = [c for c in far if c in topo.cores_of(far[0])]
    g1 = [c for c in far if c not in g0]
    rel = [c for c in topo.cores_of(core) if c not in cs and topo.die(c) == topo.die(core)
           and all(topo.may_write(c, d) for d in far)]
    srel = []
    for grp in (g0, g1):
        cand = [c for c in range(256) if topo.mates(c, grp[0]) and topo.die(c) == topo.die(core) and topo.same_plane(core, c)
                and all(topo.may_write(c, d) for d in grp)]
        users = [c for c in cs if topo.same_plane(c, cand[0]) and topo.die(c) == topo.die(core)]
        srel.append(cand[users.index(core)])
    rk = T.rank_of
    PLANS[core] = {"near": [[rk(c) for c in plane], [rk(c) for c in here]], "far": [[rk(c) for c in g0], [rk(c) for c in g1]],
                   "codes": rel[:2], "scales": srel}
    return PLANS[core]


def bits(es):
    m = 0
    for e in es:
        m |= 1 << e
    return m


def rank_program(g, core, T, topo):
    if T.rank_of(core) is None:
        relay_program(g, core, T, topo)
    else:
        home_program(g, core, T, topo)


def xfer(T, topo, src, dst, engs, sem, out, in_):
    rid, pid = topo.addr(dst, src)
    return RemoteDMATransfer(dst_ids=[DstId(rid=rid, pnc=pid)], dma_engine_mask=bits(engs), remote_sem=T.sem[sem], src=in_, dst=out)


def u8(T, name, a, b):
    return T[name][:, a:b].bitcast(dt.uint8)


def relay_program(g, core, T, topo):
    src, grp, role = None, None, None
    for c in T.cores:
        p = plan(T, topo, c)
        for i in range(2):
            for k in ("codes", "scales"):
                if p[k][i] == core:
                    src, grp, role = T.rank_of(c), p["far"][i], k
    if src is None:
        return
    sent = [0]

    def hand(wait, sem, mk):
        ts = []
        g.wait_ge(T.sem[wait], FF)
        for j, d in enumerate(grp):
            dst = T.cores[d]
            es = topo.engines(core, dst)[FR * j:FR * j + FR]
            pd = plan(T, topo, dst)
            at = (pd["far"][0] + pd["far"][1]).index(src)
            out, in_ = mk(j, at)
            ts.append(xfer(T, topo, core, dst, es, sem, out, in_))
            sent[0] += FR
        g.remote_dma_fused(ts, local_sem=T.sem.sent)

    o = 32 * src
    if role == "codes":
        hand("rzc", "azf", lambda j, at: (u8(T, "zf", 32 * at, 32 * at + 32), u8(T, "rz", 32 * j, 32 * j + 32)))
        hand("r1c", "hv1f", lambda j, at: (u8(T, "lv1", o, o + 32), u8(T, "rv1", 32 * j, 32 * j + 32)))
        hand("r2c", "hv2f", lambda j, at: (u8(T, "lv2", o, o + 32), u8(T, "rv2", 32 * j, 32 * j + 32)))
        hand("rnc", "hnf", lambda j, at: (T["lan"][:, 2 * src:2 * src + 2], T["rn"][:, 2 * j:2 * j + 2]))
    else:
        hand("rzs", "azf", lambda j, at: (T["zf_s"][:, 32 * at:32 * at + 32], T["rz_s"][:, 32 * j:32 * j + 32]))
        hand("r1s", "hv1f", lambda j, at: (T["lv1_s"][:, o:o + 32], T["rv1_s"][:, 32 * j:32 * j + 32]))
        hand("r2s", "hv2f", lambda j, at: (T["lv2_s"][:, o:o + 32], T["rv2_s"][:, 32 * j:32 * j + 32]))
    g.wait_ge(T.sem.sent, sent[0])


def home_program(g, core, T, topo):
    me = T.rank_of(core)
    pl = plan(T, topo, core)
    queue = {"v": g.vector, "s": g.scalar, "t": g.tensor, "p": g, "y": g.sync}
    engsem = {"v": "ev", "s": "es", "t": "et", "p": "ep"}
    known = {e: {} for e in queue}
    count = {e: 0 for e in queue}
    total, waited, hist = {}, {}, {}
    PS = ("sc", "dd")

    def clash(a, b):
        if a[1] >= b[2] or b[1] >= a[2]:
            return False
        s, t = (a[3] if len(a) > 3 else 1), (b[3] if len(b) > 3 else 1)
        if s > 1 and s == t and a[1] % s != b[1] % s:
            return False
        return True

    def need(e, reads, writes):
        deps = []
        for rs, wr in ((reads, False), (writes, True)):
            for r in rs:
                ps = r[0] in PS
                for (q, qw, qe, ev, clk) in hist.get(r[0], []):
                    if (wr or qw or (ps and qe != e)) and clash(r, q):
                        if ps and e == "t" and qe == "t":
                            continue
                        deps.append((ev, clk))
        best = {}
        for ev, clk in deps:
            if known[e].get(ev[0], 0) < ev[1] and (ev[0] not in best or best[ev[0]][0] < ev[1]):
                best[ev[0]] = (ev[1], clk)
        for s in list(best):
            v = best[s][0]
            if any(o != s and best[o][1].get(s, 0) >= v for o in best):
                del best[s]
        for s, (v, clk) in best.items():
            queue[e].wait_ge(T.sem[s], v)
            waited[s] = max(waited.get(s, 0), v)
            for k2, v2 in clk.items():
                known[e][k2] = max(known[e].get(k2, 0), v2)
            known[e][s] = max(known[e].get(s, 0), v)

    def note(e, reads, writes, ev, clk):
        for r in reads:
            hist.setdefault(r[0], []).append((r, False, e, ev, clk))
        for r in writes:
            hist.setdefault(r[0], []).append((r, True, e, ev, clk))

    def op(e, call, reads, writes):
        need(e, reads, writes)
        count[e] += 1
        ev = (engsem[e], count[e])
        call().then_inc(T.sem[ev[0]], 1)
        total[ev[0]] = count[e]
        clk = dict(known[e])
        clk[ev[0]] = ev[1]
        note(e, reads, writes, ev, clk)

    nl = [0]

    def dma(e, out, in_, reads, writes, store=False):
        need(e, reads, writes)
        if store:
            s = "st"
        else:
            s = "l%d" % nl[0]
            nl[0] += 1
        total[s] = total.get(s, 0) + 16
        queue[e].dma_start(out, in_).then_inc(T.sem[s], 16)
        if not store:
            clk = dict(known[e])
            clk[s] = 16
            note(e, reads, writes, (s, 16), clk)

    def arrive(sem, n, writes):
        total[sem] = n
        note("r", [], writes, (sem, n), {sem: n})

    def fused(reads, parts):
        need("p", reads, [])
        ts = [xfer(T, topo, core, d, es, sem, out, in_) for (d, es, sem, out, in_) in parts]
        total["sent"] = total.get("sent", 0) + sum(len(p[1]) for p in parts)
        g.remote_dma_fused(ts, local_sem=T.sem.sent)

    def ap(r):
        return T[r[0]][:, r[1]:r[2]:r[3]] if len(r) > 3 and r[3] > 1 else T[r[0]][:, r[1]:r[2]]

    def isr(x):
        return isinstance(x, tuple)

    def vcopy(o, i):
        op("v", lambda: g.vector.tensor_copy(ap(o), ap(i)), [i], [o])

    def vset(o, c):
        op("v", lambda: g.vector.memset(ap(o), c), [], [o])

    def vts(o, i, s1, s2, op0, op1=None):
        rd = [i] + [s for s in (s1, s2) if isr(s)]
        a1 = ap(s1) if isr(s1) else s1
        a2 = ap(s2) if isr(s2) else s2
        if op1 is None:
            op("v", lambda: g.vector.tensor_scalar(ap(o), ap(i), a1, None, op0), rd, [o])
        else:
            op("v", lambda: g.vector.tensor_scalar(ap(o), ap(i), a1, a2, op0, op1), rd, [o])

    def vtt(o, a, b, o0):
        op("v", lambda: g.vector.tensor_tensor(ap(o), ap(a), ap(b), o0), [a, b], [o])

    def vscan(o, d0, d1, init, o0, o1):
        op("v", lambda: g.vector.tensor_tensor_scan(ap(o), ap(d0), ap(d1), init, o0, o1), [d0, d1], [o])

    def vtr(o, i):
        op("v", lambda: g.vector.transpose(ap(o), ap(i)), [i], [o])

    def vsum(o, i):
        op("v", lambda: g.vector.tensor_reduce(ap(o), ap(i), AxisListType.X, OP.add), [i], [o])

    def quant(o, n0, i):
        w = (i[2] - i[1]) // 4
        a, b = (o, n0, n0 + w), (o + "_s", n0, n0 + w)
        op("v", lambda: g.vector.quantize_mx(ap(a), ap(b), ap(i)), [i], [a, b])

    def act(o, i, f, bias=None, scale=None, acc=None):
        rd, kw, wr = [i], {}, [o]
        if bias is not None:
            kw["bias"] = ap(bias) if isr(bias) else bias
            if isr(bias):
                rd.append(bias)
        if scale is not None:
            kw["scale"] = ap(scale) if isr(scale) else scale
            if isr(scale):
                rd.append(scale)
        if acc is not None:
            kw["accum_out"] = ap(acc)
            wr.append(acc)
        op("s", lambda: g.scalar.activation(ap(o), ap(i), f, **kw), rd, wr)

    def pick_codes(o, o0, win, w1, off, c0, c1):
        oc, wc, of = (o, o0, o0 + 16 * (c1 - c0)), (win, 0, w1), (off, c0, c1)
        op("v", lambda: g.vector.tensor_copy(ap(oc).bitcast(dt.uint32), ap(wc).bitcast(dt.uint32).indirect(ap(of))), [wc, of], [oc])

    def pick_scales(o, o0, win, w1, off, c0, c1):
        osn, ws, of = (o + "_s", o0, o0 + 16 * (c1 - c0)), (win + "_s", 0, w1), (off, c0, c1)
        op("s", lambda: g.scalar.activation(ap(osn), ap(ws).indirect(ap(of)), AF.Copy), [ws, of], [osn])

    def pick(*a):
        pick_codes(*a)
        pick_scales(*a)

    def mm(ps, bank, l, l0, r, r0, start=True, stop=True, n=128):
        o = (ps, 512 * bank, 512 * bank + n)
        a, sa, b, sb = (l, l0, l0 + 128), (l + "_s", l0, l0 + 128), (r, r0, r0 + n), (r + "_s", r0, r0 + n)
        op("t", lambda: g.tensor.matmul_mx(ap(o), ap(a), ap(sa), ap(b), ap(sb), start, stop), [a, sa, b, sb], [(ps, 512 * bank, 512 * bank + 512)])

    dma("y", T.xt[:, 0:512], T.x[:], [], [("xt", 0, 512)])
    dma("s", T.zb[:, 0:32], T.co[:, 0:32], [], [("zb", 0, 32)])
    dma("y", T.wt[:], T.w[:], [], [("wt", 0, 512)])

    def book(b, hs=range(4)):
        for h in hs:
            act((b + "t", 512 * h, 512 * h + 512), ("zr", 0, 512), AF.Copy)
        for h in hs:
            dma("y", T[b + "t"][32 * h:32 * h + 32, 512 * h:512 * h + 512], T[b][32 * h:32 * h + 32, :], [], [(b + "t", 512 * h, 512 * h + 512)])

    near, far = pl["near"][0] + pl["near"][1], pl["far"][0] + pl["far"][1]
    own = near.index(me)

    def both(n, a, b):
        return [(n, a, b), (n + "_s", a, b)]

    nw, hw1, hw2, nn_ = [], [], [], []
    for k, r in enumerate(near):
        if r != me:
            nw += both("zn", 32 * k, 32 * k + 32)
            hw1 += both("lv1", 32 * r, 32 * r + 32)
            hw2 += both("lv2", 32 * r, 32 * r + 32)
            nn_.append(("lan", 2 * r, 2 * r + 2))
    from_near = 2 * FN + FM
    arrive("azn", 2 * from_near, nw)
    arrive("hv1n", 2 * from_near, hw1)
    arrive("hv2n", 2 * from_near, hw2)
    arrive("hnn", from_near, nn_)
    arrive("azf", 4 * 2 * FR, both("zf", 0, 128))
    hw1, hw2, nn_ = [], [], []
    for r in far:
        hw1 += both("lv1", 32 * r, 32 * r + 32)
        hw2 += both("lv2", 32 * r, 32 * r + 32)
        nn_.append(("lan", 2 * r, 2 * r + 2))
    arrive("hv1f", 4 * 2 * FR, hw1)
    arrive("hv2f", 4 * 2 * FR, hw2)
    arrive("hnf", 4 * FR, nn_)

    def iota(o, pat, base, cm):
        if o[0] == "ip":
            op("p", lambda: g.iota(ap(o), pat, base, cm), [], [o])
        else:
            op("p", lambda: g.iota(ap(o), pat, base, cm, allow_small_or_imprecise_dtypes=True), [], [o])

    def C(k):
        return ("cf", k, k + 1)
    R16, HQ, U1, P16, P3, E0, HQ128, CHI, CLO, G, FH, T0, T1, T2, T3, T4, T5 = [C(k) for k in range(17)]
    TOK = ("tok", 0, 1)
    pf = [q[0] // 2 for q in pl["far"]]
    pn = [q[0] // 2 for q in pl["near"]]
    iota(("c256", 0, 8), [[256, 8]], 0, 0)
    iota(TOK, [[0, 1]], 0, 1)
    iota(("itr", 0, 128), [[1, 128]], 0, 0)
    iota(("ir", 0, 128), [[0, 8], [2, 16]], -15, 0)
    iota(("ict", 0, 8), [[512 * (pf[1] - pf[0]), 2], [256, 2], [32, 2]], 512 * pf[0], 0)
    iota(("ict", 8, 16), [[512 * (pn[1] - pn[0]), 2], [256, 2], [32, 2]], 512 * pn[0], 0)
    iota(("ip", 0, 1), [[1, 1]], 0, 1)
    iota(("ik", 0, 128), [[0, 2], [1, 16], [64, 4]], 0, 0)
    iota(("imx", 0, 32), [[1, 8], [0, 4]], 0, 0)

    vset(("zr", 0, 512), 0.0)
    act(("zb", 32, 544), ("zr", 0, 512), AF.Copy)
    book("b1")
    book("b2", HS0)
    vset(("xt", 512, 520), 0.0)
    vset(("le", 0, 1), 0.0)
    vset(("zt", 0, 16), 0.0)
    vset(("onb", 0, 520), 1.0)
    op("p", lambda: g.affine_select(T.gp[:, 0:520], T.onb[:, 0:520], [[-1, 520]], OP.is_equal, 0.0, 3, 4),
       [("onb", 0, 520)], [("gp", 0, 520)])
    vts(T0, TOK, -128.0, None, OP.add)
    vts(CHI, T0, M16, M16, OP.add, OP.subtract)
    vtt(CLO, T0, CHI, OP.subtract)
    vts(("tri", 0, 512, 4), ("itr", 0, 128), TOK, 2.0, OP.is_gt, OP.mult)
    vts(("tri", 1, 512, 4), ("itr", 0, 128), TOK, None, OP.is_equal)
    vset(("zb", 514, 544, 4), -15.0)
    vcopy(("zb", 513, 544, 4), ("c256", 0, 8))
    quant("qc", 0, ("zb", 0, 512))
    vts(("tri", 2, 512, 4), ("itr", 0, 128), TOK, None, OP.is_equal)
    vset(("tri", 3, 512, 4), 0.0)

    quant("qx", 0, ("xt", 0, 520))
    mm("sc", 0, "qx", 0, "qc", 0)
    quant("qtri", 0, ("tri", 0, 512))
    vscan(("pmc", 0, 8), ("zt", 0, 8), ("sc", 0, 8), BIG, OP.add, OP.max)
    vts(("le", 1, 9), ("pmc", 0, 8), ("pmc", 7, 8), None, OP.is_ge)
    vtt(("zb", 512, 544, 4), ("le", 1, 9), ("le", 0, 8), OP.subtract)
    quant("qo", 0, ("zb", 32, 544))
    mm("sc", 1, "qtri", 0, "qo", 0)
    for l in ("lv1", "lv2"):
        dma("y", u8(T, l, 256, 258), u8(T, "qx", 128, 130), [("qx", 128, 130)], [(l, 256, 258)])
        dma("y", T[l + "_s"][:, 256:258], T["qx_s"][:, 128:130], [("qx_s", 128, 130)], [(l + "_s", 256, 258)])
    vset(("sx", 2, 576, 4), 0.0)
    vset(("sx", 3, 576, 4), 0.0)
    vtt(("g8", 0, 8), ("zb", 512, 544, 4), ("sc", 632, 640), OP.mult)
    vsum(G, ("g8", 0, 8))
    vts(FH, G, M32, M32, OP.add, OP.subtract)
    vts(("sx", 0, 512, 4), ("ir", 0, 128), FH, G, OP.add, OP.is_equal)
    vts(("sx", 1, 512, 4), ("ir", 0, 128), FH, G, OP.add, OP.is_equal)
    vts(("sx", 512, 576, 4), ("ict", 0, 16), FH, CHI, OP.is_equal, OP.mult)
    vts(("sx", 513, 576, 4), ("ict", 0, 16), FH, CLO, OP.is_equal, OP.mult)
    quant("qs", 0, ("sx", 0, 576))
    mm("sc", 2, "qs", 0, "qs", 16)
    vset(("rst", 0, 256), 0.0)
    vts(("offs", 0, 16), ("sc", 1136, 1152), 128.0, None, OP.add)

    def to_relays(kind, buf, w, dstbuf, sem):
        codes = SCRATCH[buf][2] == F8
        parts = []
        for i, rc in enumerate(pl[kind]):
            es = topo.engines(core, rc)
            k = (len(es) - 2 * FF) + FF * i
            if codes:
                parts.append((rc, es[k:k + FF], sem, u8(T, dstbuf, 0, w), u8(T, buf, w * i, w * i + w)))
            else:
                parts.append((rc, es[k:k + FF], sem, T[dstbuf][:, 0:w], T[buf][:, w * i:w * i + w]))
        fused([(buf, 0, 2 * w)], parts)

    def to_near(buf, w, dstbuf, place, sem):
        codes = SCRATCH[buf][2] == F8
        parts = []
        for k, d in enumerate(near):
            if d == me:
                continue
            a, dc, n = place(d), T.cores[d], len(parts)
            es = topo.engines(core, dc)
            es = es[len(es) - FM:] if d in pl["near"][1] else es[FN * n:FN * n + FN]
            if codes:
                parts.append((dc, es, sem, u8(T, dstbuf, a, a + w), u8(T, buf, w * k, w * k + w)))
            else:
                parts.append((dc, es, sem, T[dstbuf][:, a:a + w], T[buf][:, w * k:w * k + w]))
        fused([(buf, 0, 4 * w)], parts)

    pick("sf", 0, "qx", 130, "offs", 0, 8)
    to_relays("codes", "sf", 64, "rz", "rzc")
    to_relays("scales", "sf_s", 64, "rz_s", "rzs")
    pick("sn", 0, "qx", 130, "offs", 8, 16)

    def at_near(d):
        p = plan(T, topo, T.cores[d])
        return 32 * (p["near"][0] + p["near"][1]).index(me)
    to_near("sn", 32, "zn", at_near, "azn")
    to_near("sn_s", 32, "zn_s", at_near, "azn")

    def keep(dst, d0, src, s0):
        dma("y", u8(T, dst, d0, d0 + 32), u8(T, src, s0, s0 + 32), [(src, s0, s0 + 32)], [(dst, d0, d0 + 32)])
        dma("y", T[dst + "_s"][:, d0:d0 + 32], T[src + "_s"][:, s0:s0 + 32], [(src + "_s", s0, s0 + 32)], [(dst + "_s", d0, d0 + 32)])
    keep("zn", 32 * own, "sn", 32 * own)
    book("b2", HS1)
    act(("gm", 0, 520), ("gp", 0, 520), AF.Copy, scale=-1.0)

    for k, (sh, m) in enumerate(((0, 15), (5, 7), (4, 1), (4, 7), (0, 3))):
        o = ("ic", k, k + 1)
        if sh:
            vts(o, ("ip", 0, 1), sh, m, OP.arith_shift_right, OP.bitwise_and)
        else:
            vts(o, ("ip", 0, 1), m, None, OP.bitwise_and)
    vcopy(("cf", 0, 5), ("ic", 0, 5))
    vts(HQ128, HQ, 128.0, None, OP.mult)
    vts(E0, U1, -1.0, 1.0, OP.mult, OP.add)
    vset(("rst", 0, 256, 128), BIG)
    for h in range(4):
        vts(("w16", 128 * h, 128 * h + 128), ("ik", 0, 128), -64.0 * h, R16, OP.add, OP.is_equal)
    quant("qw16", 0, ("w16", 0, 512))
    vts(("mxx", 0, 32), ("imx", 0, 32), P16, None, OP.is_equal)
    vts(("offc", 0, 2), ("zt", 0, 2), P3, None, OP.add)
    vset(("xb", 64, 544), 0.0)

    def relocate(x, n4, bank):
        ql, v = "ql" + x, (544 if x == "n" else 0)
        o, w, f, m = ("xm" + x, 0, 32), (n4, 0, 4), ("offc", 0, 2), ("mxx", 0, 32)
        a = 64 if x == "n" else 0
        k = 512 * bank + (120 if x == "n" else 0)

        def spread():
            op("v", lambda: g.vector.tensor_tensor(ap(o), ap(w).indirect(ap(f)), ap(m), OP.mult), [w, f, m], [o])

        def products():
            mm("sc", bank, "qw16", 0, ql, 0, True, False)
            mm("sc", bank, "qw16", 0, ql, 8, False, True)
        return (spread, lambda: vts(("xb", v, v + 32), o, M16, M16, OP.add, OP.subtract),
                lambda: vtt(("xb", v + 32, v + 64), o, ("xb", v, v + 32), OP.subtract),
                lambda: quant(ql, 0, ("xb", a, a + 544)), products), ("sc", k, k + 8)

    def home_list():
        vts(T0, G, -112.0, M256, OP.add, OP.add)
        vts(T1, T0, M256, 0.25, OP.subtract, OP.mult)
        vts(T2, T1, -4.0, G, OP.mult, OP.add)
        vts(T3, T2, 2.0 * CAPP - 16, 0.5, OP.is_lt, OP.mult)
        vts(T4, T2, T1, 15.0 - 512.0, OP.add, OP.add)
        vtt(T5, T4, T3, OP.mult)
        vts(("n4h", 0, 4), ("zt", 0, 4), T5, None, OP.add)
        fs, ls = relocate("n", "n4h", 3)
        for f in fs:
            f()
        vts(("offh", 0, 8), ls, 256.0, None, OP.add)

    def level(x, l):
        win, bk, pm, n4, nn, off, sa = ("z" if l == 1 else "rq") + x, "qb%d" % l, "pm" + x, "n4" + x, "nn" + x, "off%d%s" % (l, x), "sa" + x
        b0 = 0 if x == "n" else 2
        fs, ls = relocate(x, n4, b0)
        a, b = ls[1], ls[2]
        v = ("v%d%s" % (l, x), 0, bk, 512, off, 0, 8)

        def score():
            for i in range(2):
                mm("sc", b0 + i, win, 0, bk, 256 * i, True, True, 256)

        def scan(i):
            k = 512 * (b0 + i)
            vscan((pm, 256 * i, 256 * i + 256), ("rst", 0, 256), ("sc", k, k + 256), 0.0, OP.add, OP.max)

        def tally(i):
            for h in range(2 * i, 2 * i + 2):
                act(("jk", 128 * h, 128 * h + 128), (pm, 128 * h, 128 * h + 128), AF.Sign, bias=(pm, 128 * h + 127, 128 * h + 128),
                    scale=-1.0, acc=(n4, h, h + 1))

        def parts():
            act((sa, 0, 4), ("sc", a, b, 2), AF.Copy, scale=E0)
            act((sa, 4, 8), ("sc", a + 1, b, 2), AF.Copy, scale=U1)

        d = {"place%d" % i: f for i, f in enumerate(fs)}
        for i in range(2):
            d.update({"scan%d" % i: lambda i=i: scan(i), "count%d" % i: lambda i=i: tally(i)})
        d.update({"score": score, "list": lambda: vts((off, 0, 8), ls, HQ128, None, OP.add), "codes": lambda: pick_codes(*v),
                  "scales": lambda: pick_scales(*v), "parts": parts,
                  "number": lambda: vtt((nn, l - 1, 8, 2), (sa, 0, 4), (sa, 4, 8), OP.add),
                  "codesback": lambda: back(x, l, True), "scalesback": lambda: back(x, l, False)})
        return d

    def back(x, l, codes):
        v, lv = "v%d%s" % (l, x), "lv%d" % l
        if x == "f" and codes:
            to_relays("codes", v, 64, "rv%d" % l, "r%dc" % l)
        elif x == "f":
            to_relays("scales", v + "_s", 64, "rv%d_s" % l, "r%ds" % l)
        elif codes:
            to_near(v, 32, lv, lambda d: 32 * me, "hv%dn" % l)
        else:
            to_near(v + "_s", 32, lv + "_s", lambda d: 32 * me, "hv%dn" % l)
            keep(lv, 32 * me, v, 32 * own)

    def given(x):
        for b in range(4):
            mm("dd", b, "qe", 128 * b, "z" + x, 0, True, False)

    def minus(x):
        for b in range(4):
            mm("dd", b, "qm", 128 * b, "v1" + x, 0, False, True)

    def rest(x, b):
        o, i = ("rt" + x, b, 512, 4), ("dd", 512 * b, 512 * b + 128)
        if b % 2:
            act(o, i, AF.Copy)
        else:
            vcopy(o, i)

    def near_numbers():
        to_near("nnn", 2, "lan", lambda d: 2 * me, "hnn")
        dma("y", T.lan[:, 2 * me:2 * me + 2], T.nnn[:, 2 * own:2 * own + 2], [("nnn", 2 * own, 2 * own + 2)], [("lan", 2 * me, 2 * me + 2)])

    def last():
        vset(("xw", 0, 256), 0.0)
        vset(("xtw", 256, 288), -1.0)

    def steps():
        d = {}
        for x in "nf":
            for l in (1, 2):
                d.update({"%s%d.%s" % (x.upper(), l, n): f for n, f in level(x, l).items()})
            d.update({x + ".given": lambda x=x: given(x), x + ".minus": lambda x=x: minus(x),
                      x + ".repack": lambda x=x: quant("rq" + x, 0, ("rt" + x, 0, 512))})
            for b in range(4):
                d[x + ".rest%d" % b] = lambda x=x, b=b: rest(x, b)
        for b in range(4):
            d["qe%d" % b] = lambda b=b: quant("qe", 128 * b, ("gp", 3 - b, 515 - b))
            d["qm%d" % b] = lambda b=b: quant("qm", 128 * b, ("gm", 3 - b, 515 - b))
        d.update({"hl": home_list, "fin": last,
                  "qb1": lambda: quant("qb1", 0, ("b1t", 0, 2048)), "qb2": lambda: quant("qb2", 0, ("b2t", 0, 2048)),
                  "qw": lambda: quant("qw", 0, ("wt", 0, 512)), "f.nums": lambda: to_relays("codes", "nnf", 4, "rn", "rnc"),
                  "n.nums": near_numbers})
        return d

    todo = steps()
    for name in ORDER.split():
        todo[name]()

    def store(l):
        h = "h%d" % l
        o = 128 * (l - 1)
        dma("y", T.oc[:, 4 * o:4 * o + 512], u8(T, h, 0, 128), [(h, 0, 128)], [], True)
        for k in range(4):
            dma("y" if k % 2 else "s", T.osc[4 * k:4 * k + 4, o:o + 128], T[h + "_s"][32 * k:32 * k + 4, 0:128], [(h + "_s", 0, 128)], [], True)

    pick("h1", 0, "lv1", 258, "offh", 0, 8)
    store(1)
    mm("sc", 3, "qw", 0, "h1", 0, True, False)
    pick("h2", 0, "lv2", 258, "offh", 0, 8)
    mm("sc", 3, "qw", 0, "h2", 0, False, True)
    store(2)
    for l in range(2):
        vcopy(("xw", l, 256, 32), ("lan", l, 16, 2))
    vtr(("xtw", 0, 256), ("xw", 0, 256))
    act(("yt", 0, 128), ("sc", 1536, 1664), AF.Copy)
    dma("s", T.y[:], T.yt[:], [("yt", 0, 128)], [], True)
    o, w, f = ("wnt", 0, 128), ("xtw", 0, 288), ("offh", 0, 8)
    op("v", lambda: g.vector.tensor_copy(ap(o), ap(w).indirect(ap(f))), [w, f], [o])
    for l in range(2):
        dma("ys"[l], T.wn[4 * l:4 * l + 4, :], T.wnt[l:128:32, 0:128], [o], [], True)
    for s in total:
        if waited.get(s, 0) < total[s]:
            g.wait_ge(T.sem[s], total[s])
